import numpy as np
import ml_dtypes


def mxq(x, axis, fmt="e4m3"):
    dtype, down = {"e4m3": (ml_dtypes.float8_e4m3fn, 7), "e5m2": (ml_dtypes.float8_e5m2, 14)}[fmt]
    v = np.moveaxis(np.asarray(x, np.float32).astype(ml_dtypes.bfloat16).astype(np.float64), axis, -1)
    blocks = v.reshape(v.shape[:-1] + (-1, 32))
    amax = np.abs(blocks).max(-1, keepdims=True)
    byte = np.maximum(np.where(amax > 0, np.frexp(amax)[1] - 1 + 127, 0) - down, 1)
    scale = np.exp2(byte - 127.0)
    codes = (blocks / scale).astype(np.float32).astype(dtype).astype(np.float64)
    return np.moveaxis((codes * scale).reshape(v.shape), -1, axis)


WIDE = False


def mx_kscale(k):
    if not WIDE:
        return np.ones(k)
    levels = np.array([10, -10, 5, -5, 0])
    if k % 512:
        return np.exp2(np.random.permutation(np.resize(levels, k // 32))).repeat(32)
    a = np.empty((k // 512, 16))
    for p in range(k // 512):
        a[p, :8] = np.random.permutation(np.resize(levels, 8))
        for g in range(8):
            far = levels[np.abs(levels - a[p, g]) >= 10]
            a[p, g + 8] = far[np.random.randint(len(far))]
    return np.exp2(a.ravel()).repeat(32)


def f64(x):
    return np.asarray(x).astype(np.float64)


def striped(idx):
    return np.tile(idx.reshape(-1, 16).T, (8, 1)).astype(np.uint16)


def unstriped(offs):
    return offs[:16].T.reshape(-1).astype(np.int64)


def gelu(v):
    return 0.5 * v * (1.0 + np.tanh(np.sqrt(2.0 / np.pi) * (v + 0.044715 * v**3)))


K, T, E, C, N = 2048, 512, 8, 128, 128


def by_expert(wq, xq):
    return np.concatenate([wq[e].T @ xq[:, e * C:(e + 1) * C] for e in range(E)], axis=1)


def setup_inputs():
    n = np.random.standard_normal
    s = mx_kscale(K)[:, None]
    first = np.random.permutation(np.repeat(np.arange(E), T // E))
    second = (first + 1 + np.random.permutation(np.repeat(np.arange(E - 1), -(-T // (E - 1)))[:T])) % E
    while np.bincount(second, minlength=E).max() != T // E:
        load = np.bincount(second, minlength=E); hi, lo = int(load.argmax()), int(load.argmin())
        t = np.flatnonzero((second == hi) & (first != lo))[0]; second[t] = lo
    slot_token = np.empty(E * C, np.int64); pos = np.empty((2, T), np.int64); fill = np.zeros(E, np.int64)
    place = np.stack([np.random.permutation(C) for _ in range(E)])
    for r, deal in enumerate((first, second)):
        for t in np.random.permutation(T):
            e = deal[t]; j = e * C + place[e, fill[e]]; fill[e] += 1; slot_token[j] = t; pos[r, t] = j
    g = np.random.uniform(0.2, 0.8, T)
    return {
        "xT": (n((K, T)) * s).astype(np.float32),
        "w": (n((E, K, N)) / np.sqrt(K) / s[None]).astype(np.float32),
        "b": (0.3 * n((N, E))).astype(np.float32),
        "gate": np.stack([np.tile(g, (N, 1)), np.tile(1.0 - g, (N, 1))]).astype(np.float32),
        "offs": striped(slot_token),
        "pos1": striped(pos[0]),
        "pos2": striped(pos[1]),
    }


def reference(xT, w, b, gate, offs, pos1, pos2):
    idx = unstriped(offs)
    xq = mxq(f64(xT)[:, idx], 0, "e4m3")
    y = by_expert(mxq(f64(w), 1, "e4m3"), xq)
    y = gelu(y + np.repeat(f64(b), C, axis=1))
    return f64(gate[0]) * y[:, unstriped(pos1)] + f64(gate[1]) * y[:, unstriped(pos2)]

@@ -1,0 +1,175 @@
+from contextlib import ExitStack
+
+import concourse.mybir as mybir
+
+K, T, E, C, N = 2048, 512, 8, 128, 128
+FLOPS = 2 * K * N * E * C
+
+F32 = mybir.dt.float32
+BF16 = mybir.dt.bfloat16
+U32 = mybir.dt.uint32
+U16 = mybir.dt.uint16
+U8 = mybir.dt.uint8
+FP8X4 = mybir.dt.float8_e4m3fn_x4
+MULT = mybir.AluOpType.mult
+ADD = mybir.AluOpType.add
+GELU = mybir.ActivationFunctionType.Gelu_apprx_tanh
+
+P = 128
+G = 4
+S = E * C
+HALF = 512
+PAD = 32
+
+V_E = ()
+
+
+def tile_routed_moe_kernel(tc, xT, w, b, gate, offs, pos1, pos2, out):
+    nc = tc.nc
+    with ExitStack() as ctx:
+        lists = ctx.enter_context(tc.tile_pool(name="lists", bufs=1))
+        keep = ctx.enter_context(tc.tile_pool(name="keep", bufs=1))
+        ring = ctx.enter_context(tc.tile_pool(name="ring", bufs=3))
+        psum = ctx.enter_context(tc.psum_pool(name="psum", bufs=1))
+
+        offs_t = lists.tile([P, S // 16], U16, name="offs_t")
+        pos1_t = lists.tile([P, T // 16], U16, name="pos1_t")
+        pos2_t = lists.tile([P, T // 16], U16, name="pos2_t")
+
+        xp = [[keep.tile([P, T + PAD], F32, name="xp%d%d" % (g, t)) for t in range(4)] for g in range(G)]
+        wr = [keep.tile([P, G, 4 * N], F32, name="wr%d" % e) for e in range(E)]
+        xc = keep.tile([P, G, S], U32, name="xc", align_bytes=64)
+        xs = keep.tile([P, G, S], U8, name="xs", align_bytes=64)
+        wc = keep.tile([P, E, G * N], U32, name="wc", align_bytes=64)
+        ws = keep.tile([P, E, G * N], U8, name="ws", align_bytes=64)
+        b_t = keep.tile([P, E], F32, name="b_t")
+        gate0 = keep.tile([P, T], F32, name="gate0")
+        gate1 = keep.tile([P, T], F32, name="gate1")
+        y = keep.tile([P, S], F32, name="y")
+        acc = [psum.tile([P, C], F32, name="acc%d" % e) for e in range(E)]
+
+        xv = xT.rearrange("(g p t) n -> g p t n", p=P, t=4)
+        wv = w.rearrange("e (g p t) n -> e p g (t n)", p=P, t=4)
+
+        def load_x(g):
+            for t in range(4):
+                nc.sync.dma_start(out=xp[g][t][:, 0:T], in_=xv[g, :, t, :])
+
+        def load_w(e):
+            nc.sync.dma_start(out=wr[e][:], in_=wv[e])
+
+        nc.sync.dma_start(offs_t[:], offs)
+        load_x(0)
+        load_w(0)
+        load_w(1)
+        load_x(1)
+        load_w(2)
+        load_w(3)
+        load_x(2)
+        load_w(4)
+        load_w(5)
+        load_x(3)
+        nc.sync.dma_start(pos1_t[:], pos1)
+        nc.sync.dma_start(pos2_t[:], pos2)
+        nc.sync.dma_start(out=b_t[:], in_=b)
+        load_w(6)
+        load_w(7)
+        nc.sync.dma_start(out=gate0[:], in_=gate[0])
+        nc.sync.dma_start(out=gate1[:], in_=gate[1])
+
+        warm = keep.tile([P, 1], F32, name="warm")
+        warm2 = keep.tile([P, 1], F32, name="warm2")
+        nc.gpsimd.memset(warm[:], 0.0)
+        nc.scalar.activation(out=warm2[:], in_=warm[:], func=GELU)
+        for g in range(G):
+            for t in range(4):
+                nc.gpsimd.memset(xp[g][t][:, T : T + PAD], 0.0)
+
+        def copy_on(vector, dst, src):
+            if vector:
+                nc.vector.tensor_copy(out=dst, in_=src)
+            else:
+                nc.scalar.copy(out=dst, in_=src)
+
+        gathered = {}
+        grouped = {}
+        w_grouped = {}
+        done_x = []
+        done_w = []
+        issued = {}
+
+        def gather(i):
+            g, h = divmod(i, 2)
+            gt = ring.tile([P, 4, HALF], F32, name="gt")
+            gathered[i] = gt
+            col = h * HALF // 16
+            for t in range(4):
+                nc.vector.tensor_copy(gt[:, t, :], xp[g][t][:].indirect(offs_t[:, col : col + HALF // 16]))
+
+        def interleave(i):
+            qt = ring.tile([P, 4 * HALF], BF16, name="qt", align_bytes=64)
+            grouped[i] = qt
+            copy_on(False, qt[:].rearrange("p (j t) -> p j t", t=4), gathered[i][:].rearrange("p t j -> p j t"))
+
+        def matmuls():
+            for (g, h) in done_x:
+                for e in done_w:
+                    if e // 4 != h or (e, g) in issued:
+                        continue
+                    count = len([1 for key in issued if key[0] == e])
+                    issued[(e, g)] = True
+                    nc.tensor.matmul_mx(
+                        out=acc[e][:],
+                        lhsT=wc[:, e, g * N : (g + 1) * N].bitcast(FP8X4),
+                        lhsT_scale=ws[:, e, g * N : (g + 1) * N],
+                        rhs=xc[:, g, e * C : (e + 1) * C].bitcast(FP8X4),
+                        rhs_scale=xs[:, g, e * C : (e + 1) * C],
+                        start=(count == 0),
+                        stop=(count == G - 1),
+                    )
+                    if count == G - 1:
+                        nc.scalar.activation(
+                            out=y[:, e * C : (e + 1) * C], in_=acc[e][:], func=GELU, bias=b_t[:, e : e + 1]
+                        )
+
+        def quantize_x(i):
+            g, h = divmod(i, 2)
+            cols = slice(h * HALF, (h + 1) * HALF)
+            nc.vector.quantize_mx(out=xc[:, g, cols].bitcast(FP8X4), scales=xs[:, g, cols], in_=grouped[i][:])
+            done_x.append((g, h))
+            matmuls()
+
+        def interleave_w(e):
+            wq = ring.tile([P, G, 4 * N], BF16, name="wq", align_bytes=64)
+            w_grouped[e] = wq
+            for a in range(2):
+                copy_on(
+                    (e, a) in V_E,
+                    wq[:, 2 * a : 2 * a + 2, :].rearrange("p g (n t) -> p g n t", t=4),
+                    wr[e][:, 2 * a : 2 * a + 2, :].rearrange("p g (t n) -> p g n t", t=4),
+                )
+
+        def quantize_w(e):
+            nc.vector.quantize_mx(
+                out=wc[:, e, :].bitcast(FP8X4), scales=ws[:, e, :], in_=w_grouped[e][:].rearrange("p g c -> p (g c)")
+            )
+            done_w.append(e)
+            matmuls()
+
+        for i in range(2 * G):
+            gather(i)
+            interleave_w(i)
+            interleave(i)
+            if i >= 1:
+                quantize_x(i - 1)
+                quantize_w(i - 1)
+        quantize_w(2 * G - 1)
+        quantize_x(2 * G - 1)
+
+        t1 = keep.tile([P, T], F32, name="t1")
+        t2 = keep.tile([P, T], F32, name="t2")
+        res = keep.tile([P, T], F32, name="res")
+        nc.vector.tensor_tensor(t1[:], y[:].indirect(pos1_t[:]), gate0[:], MULT)
+        nc.vector.tensor_tensor(t2[:], y[:].indirect(pos2_t[:]), gate1[:], MULT)
+        nc.vector.tensor_tensor(res[:], t1[:], t2[:], ADD)
+        nc.sync.dma_start(out=out, in_=res[:])

@@ -14,6 +14,7 @@ FP8X4 = mybir.dt.float8_e4m3fn_x4
 MULT = mybir.AluOpType.mult
 ADD = mybir.AluOpType.add
 GELU = mybir.ActivationFunctionType.Gelu_apprx_tanh
+COPY = mybir.ActivationFunctionType.Copy
 
 P = 128
 G = 4
@@ -21,7 +22,13 @@ S = E * C
 HALF = 512
 PAD = 32
 
-V_E = ()
+V_UNITS = ((0, 0), (0, 1), (1, 0), (1, 1), (2, 0))
+S_STEPS = (
+    ("f", 3, 0), ("i", 0), ("f", 3, 1), ("f", 3, 2), ("i", 1), ("f", 3, 3), ("i", 2), ("f", 3, 4), ("i", 3),
+    ("f", 3, 5), ("f", 3, 6), ("f", 3, 7), ("f", 2, 4), ("f", 2, 5), ("f", 2, 6), ("f", 2, 7),
+)
+V_INTERLEAVES = (4,)
+W_PIECE = 2
 
 
 def tile_routed_moe_kernel(tc, xT, w, b, gate, offs, pos1, pos2, out):
@@ -36,8 +43,15 @@ def tile_routed_moe_kernel(tc, xT, w, b, gate, offs, pos1, pos2, out):
         pos1_t = lists.tile([P, T // 16], U16, name="pos1_t")
         pos2_t = lists.tile([P, T // 16], U16, name="pos2_t")
 
-        xp = [[keep.tile([P, T + PAD], F32, name="xp%d%d" % (g, t)) for t in range(4)] for g in range(G)]
-        wr = [keep.tile([P, G, 4 * N], F32, name="wr%d" % e) for e in range(E)]
+        xp = [[keep.tile([P, T + PAD], F32, name="xp%d%d" % (g, t)) for t in range(4)] for g in range(3)]
+        xraw = keep.tile([P, 4, T], F32, name="xraw")
+        xb = {g: keep.tile([P, 4, T], BF16, name="xb%d" % g) for g in (2, 3)}
+        qs = {
+            (g, h): keep.tile([P, HALF, 4], BF16, name="qs%d%d" % (g, h), align_bytes=64)
+            for (g, h) in ((3, 0), (3, 1), (2, 1))
+        }
+        qt = [keep.tile([P, 4 * HALF], BF16, name="qt%d" % i, align_bytes=64) for i in range(len(V_UNITS))]
+        wq = [keep.tile([P, G, 4 * N], BF16, name="wq%d" % e, align_bytes=64) for e in range(E)]
         xc = keep.tile([P, G, S], U32, name="xc", align_bytes=64)
         xs = keep.tile([P, G, S], U8, name="xs", align_bytes=64)
         wc = keep.tile([P, E, G * N], U32, name="wc", align_bytes=64)
@@ -50,30 +64,30 @@ def tile_routed_moe_kernel(tc, xT, w, b, gate, offs, pos1, pos2, out):
 
         xv = xT.rearrange("(g p t) n -> g p t n", p=P, t=4)
         wv = w.rearrange("e (g p t) n -> e p g (t n)", p=P, t=4)
+        wr = {}
 
-        def load_x(g):
-            for t in range(4):
+        def load_x(g, planes):
+            for t in planes:
                 nc.sync.dma_start(out=xp[g][t][:, 0:T], in_=xv[g, :, t, :])
 
         def load_w(e):
+            wr[e] = ring.tile([P, G, 4 * N], F32, name="wr", bufs=5)
             nc.sync.dma_start(out=wr[e][:], in_=wv[e])
 
         nc.sync.dma_start(offs_t[:], offs)
-        load_x(0)
+        load_x(0, (0, 1))
+        nc.sync.dma_start(out=xraw[:], in_=xv[3])
+        load_x(0, (2, 3))
         load_w(0)
+        load_x(1, (0, 1, 2, 3))
         load_w(1)
-        load_x(1)
         load_w(2)
+        load_x(2, (0, 1, 2, 3))
         load_w(3)
-        load_x(2)
         load_w(4)
-        load_w(5)
-        load_x(3)
         nc.sync.dma_start(pos1_t[:], pos1)
         nc.sync.dma_start(pos2_t[:], pos2)
         nc.sync.dma_start(out=b_t[:], in_=b)
-        load_w(6)
-        load_w(7)
         nc.sync.dma_start(out=gate0[:], in_=gate[0])
         nc.sync.dma_start(out=gate1[:], in_=gate[1])
 
@@ -81,25 +95,17 @@ def tile_routed_moe_kernel(tc, xT, w, b, gate, offs, pos1, pos2, out):
         warm2 = keep.tile([P, 1], F32, name="warm2")
         nc.gpsimd.memset(warm[:], 0.0)
         nc.scalar.activation(out=warm2[:], in_=warm[:], func=GELU)
-        for g in range(G):
+        for g in range(3):
             for t in range(4):
                 nc.gpsimd.memset(xp[g][t][:, T : T + PAD], 0.0)
 
-        def copy_on(vector, dst, src):
-            if vector:
-                nc.vector.tensor_copy(out=dst, in_=src)
-            else:
-                nc.scalar.copy(out=dst, in_=src)
-
         gathered = {}
-        grouped = {}
-        w_grouped = {}
         done_x = []
         done_w = []
         issued = {}
 
         def gather(i):
-            g, h = divmod(i, 2)
+            g, h = V_UNITS[i]
             gt = ring.tile([P, 4, HALF], F32, name="gt")
             gathered[i] = gt
             col = h * HALF // 16
@@ -107,14 +113,26 @@ def tile_routed_moe_kernel(tc, xT, w, b, gate, offs, pos1, pos2, out):
                 nc.vector.tensor_copy(gt[:, t, :], xp[g][t][:].indirect(offs_t[:, col : col + HALF // 16]))
 
         def interleave(i):
-            qt = ring.tile([P, 4 * HALF], BF16, name="qt", align_bytes=64)
-            grouped[i] = qt
-            copy_on(False, qt[:].rearrange("p (j t) -> p j t", t=4), gathered[i][:].rearrange("p t j -> p j t"))
+            dst = qt[i][:].rearrange("p (j t) -> p j t", t=4)
+            src = gathered[i][:].rearrange("p t j -> p j t")
+            if i in V_INTERLEAVES:
+                nc.vector.tensor_copy(out=dst, in_=src)
+            else:
+                nc.scalar.copy(out=dst, in_=src)
+
+        def scalar_gather(g, e):
+            h, c = divmod(e, 4)
+            for t in range(4):
+                nc.scalar.activation(
+                    qs[(g, h)][:, c * C : (c + 1) * C, t],
+                    xb[g][:, t, :].indirect(offs_t[:, e * C // 16 : (e + 1) * C // 16]),
+                    COPY,
+                )
 
         def matmuls():
-            for (g, h) in done_x:
+            for (g, e0, e1) in done_x:
                 for e in done_w:
-                    if e // 4 != h or (e, g) in issued:
+                    if e < e0 or e >= e1 or (e, g) in issued:
                         continue
                     count = len([1 for key in issued if key[0] == e])
                     issued[(e, g)] = True
@@ -132,39 +150,61 @@ def tile_routed_moe_kernel(tc, xT, w, b, gate, offs, pos1, pos2, out):
                             out=y[:, e * C : (e + 1) * C], in_=acc[e][:], func=GELU, bias=b_t[:, e : e + 1]
                         )
 
-        def quantize_x(i):
-            g, h = divmod(i, 2)
-            cols = slice(h * HALF, (h + 1) * HALF)
-            nc.vector.quantize_mx(out=xc[:, g, cols].bitcast(FP8X4), scales=xs[:, g, cols], in_=grouped[i][:])
-            done_x.append((g, h))
+        def quantize_x(g, e0, e1, src):
+            cols = slice(e0 * C, e1 * C)
+            nc.vector.quantize_mx(out=xc[:, g, cols].bitcast(FP8X4), scales=xs[:, g, cols], in_=src)
+            done_x.append((g, e0, e1))
             matmuls()
 
         def interleave_w(e):
-            wq = ring.tile([P, G, 4 * N], BF16, name="wq", align_bytes=64)
-            w_grouped[e] = wq
-            for a in range(2):
-                copy_on(
-                    (e, a) in V_E,
-                    wq[:, 2 * a : 2 * a + 2, :].rearrange("p g (n t) -> p g n t", t=4),
-                    wr[e][:, 2 * a : 2 * a + 2, :].rearrange("p g (t n) -> p g n t", t=4),
+            for g in range(0, G, W_PIECE):
+                nc.gpsimd.tensor_scalar(
+                    wq[e][:, g : g + W_PIECE, :].rearrange("p g (n t) -> p g n t", t=4),
+                    wr[e][:, g : g + W_PIECE, :].rearrange("p g (t n) -> p g n t", t=4),
+                    1.0,
+                    0.0,
+                    MULT,
+                    ADD,
                 )
 
         def quantize_w(e):
             nc.vector.quantize_mx(
-                out=wc[:, e, :].bitcast(FP8X4), scales=ws[:, e, :], in_=w_grouped[e][:].rearrange("p g c -> p (g c)")
+                out=wc[:, e, :].bitcast(FP8X4), scales=ws[:, e, :], in_=wq[e][:].rearrange("p g c -> p (g c)")
             )
             done_w.append(e)
             matmuls()
 
-        for i in range(2 * G):
+        for e in range(3):
+            interleave_w(e)
+        for t in range(4):
+            nc.gpsimd.tensor_scalar(xb[2][:, t, :], xp[2][t][:, 0:T], 1.0, 0.0, MULT, ADD)
+        for e in range(3, E):
+            if e >= 5:
+                load_w(e)
+            interleave_w(e)
+
+        for i in range(len(V_UNITS)):
             gather(i)
-            interleave_w(i)
+
+        nc.scalar.copy(out=xb[3][:], in_=xraw[:])
+        for step in S_STEPS:
+            if step[0] == "f":
+                scalar_gather(step[1], step[2])
+            else:
+                interleave(step[1])
+        for i in V_INTERLEAVES:
             interleave(i)
-            if i >= 1:
-                quantize_x(i - 1)
-                quantize_w(i - 1)
-        quantize_w(2 * G - 1)
-        quantize_x(2 * G - 1)
+
+        for i in range(len(V_UNITS)):
+            g, h = V_UNITS[i]
+            quantize_x(g, 4 * h, 4 * h + 4, qt[i][:])
+        quantize_x(3, 0, 4, qs[(3, 0)][:].rearrange("p j t -> p (j t)"))
+        for e in range(E):
+            quantize_w(e)
+        quantize_x(3, 4, 8, qs[(3, 1)][:].rearrange("p j t -> p (j t)"))
+        flat = qs[(2, 1)][:].rearrange("p j t -> p (j t)")
+        quantize_x(2, 4, 6, flat[:, 0 : 8 * C])
+        quantize_x(2, 6, 8, flat[:, 8 * C : 16 * C])
 
         t1 = keep.tile([P, T], F32, name="t1")
         t2 = keep.tile([P, T], F32, name="t2")

@@ -23,12 +23,15 @@ HALF = 512
 PAD = 32
 
 V_UNITS = ((0, 0), (0, 1), (1, 0), (1, 1), (2, 0))
-S_STEPS = (
-    ("f", 3, 0), ("i", 0), ("f", 3, 1), ("f", 3, 2), ("i", 1), ("f", 3, 3), ("i", 2), ("f", 3, 4), ("i", 3),
-    ("f", 3, 5), ("f", 3, 6), ("f", 3, 7), ("f", 2, 4), ("f", 2, 5), ("f", 2, 6), ("f", 2, 7),
+V_INTERLEAVES = (3, 4)
+G_INTERLEAVES = (0, 1)
+X_LOADS = (
+    (0, 0, 0), (3, 0, 0), (0, 1, 0), (0, 2, 1), (0, 3, 2), (3, 1, 4), (3, 2, 10), (1, 0, 10),
+    (1, 1, 11), (1, 2, 12), (1, 3, 13), (3, 3, 13), (2, 0, 14), (2, 1, 15), (2, 2, 16), (2, 3, 17),
 )
-V_INTERLEAVES = (4,)
-W_PIECE = 2
+G_BEFORE = {5: 0, 9: 1}
+W_BUFS = 16
+GT_BUFS = 4
 
 
 def tile_routed_moe_kernel(tc, xT, w, b, gate, offs, pos1, pos2, out):
@@ -63,28 +66,26 @@ def tile_routed_moe_kernel(tc, xT, w, b, gate, offs, pos1, pos2, out):
         acc = [psum.tile([P, C], F32, name="acc%d" % e) for e in range(E)]
 
         xv = xT.rearrange("(g p t) n -> g p t n", p=P, t=4)
-        wv = w.rearrange("e (g p t) n -> e p g (t n)", p=P, t=4)
+        wv = w.rearrange("e (g p t) n -> e g p (t n)", p=P, t=4)
         wr = {}
 
-        def load_x(g, planes):
-            for t in planes:
-                nc.sync.dma_start(out=xp[g][t][:, 0:T], in_=xv[g, :, t, :])
-
-        def load_w(e):
-            wr[e] = ring.tile([P, G, 4 * N], F32, name="wr", bufs=5)
-            nc.sync.dma_start(out=wr[e][:], in_=wv[e])
+        def load_w(piece):
+            wr[piece] = ring.tile([P, 4 * N], F32, name="wr", bufs=W_BUFS)
+            nc.sync.dma_start(out=wr[piece][:], in_=wv[piece // G, piece % G])
 
         nc.sync.dma_start(offs_t[:], offs)
-        load_x(0, (0, 1))
-        nc.sync.dma_start(out=xraw[:], in_=xv[3])
-        load_x(0, (2, 3))
-        load_w(0)
-        load_x(1, (0, 1, 2, 3))
-        load_w(1)
-        load_w(2)
-        load_x(2, (0, 1, 2, 3))
-        load_w(3)
-        load_w(4)
+        loaded = 0
+        for (g, t, before) in X_LOADS:
+            while loaded < before:
+                load_w(loaded)
+                loaded += 1
+            if g == 3:
+                nc.sync.dma_start(out=xraw[:, t, :], in_=xv[g, :, t, :])
+            else:
+                nc.sync.dma_start(out=xp[g][t][:, 0:T], in_=xv[g, :, t, :])
+        while loaded < E * G:
+            load_w(loaded)
+            loaded += 1
         nc.sync.dma_start(pos1_t[:], pos1)
         nc.sync.dma_start(pos2_t[:], pos2)
         nc.sync.dma_start(out=b_t[:], in_=b)
@@ -106,7 +107,7 @@ def tile_routed_moe_kernel(tc, xT, w, b, gate, offs, pos1, pos2, out):
 
         def gather(i):
             g, h = V_UNITS[i]
-            gt = ring.tile([P, 4, HALF], F32, name="gt")
+            gt = ring.tile([P, 4, HALF], F32, name="gt", bufs=GT_BUFS)
             gathered[i] = gt
             col = h * HALF // 16
             for t in range(4):
@@ -117,17 +118,21 @@ def tile_routed_moe_kernel(tc, xT, w, b, gate, offs, pos1, pos2, out):
             src = gathered[i][:].rearrange("p t j -> p j t")
             if i in V_INTERLEAVES:
                 nc.vector.tensor_copy(out=dst, in_=src)
+            elif i in G_INTERLEAVES:
+                for c in range(4):
+                    nc.gpsimd.tensor_scalar(
+                        dst[:, c * C : (c + 1) * C, :], src[:, c * C : (c + 1) * C, :], 1.0, 0.0, MULT, ADD
+                    )
             else:
                 nc.scalar.copy(out=dst, in_=src)
 
-        def scalar_gather(g, e):
+        def scalar_gather(g, t, e):
             h, c = divmod(e, 4)
-            for t in range(4):
-                nc.scalar.activation(
-                    qs[(g, h)][:, c * C : (c + 1) * C, t],
-                    xb[g][:, t, :].indirect(offs_t[:, e * C // 16 : (e + 1) * C // 16]),
-                    COPY,
-                )
+            nc.scalar.activation(
+                qs[(g, h)][:, c * C : (c + 1) * C, t],
+                xb[g][:, t, :].indirect(offs_t[:, e * C // 16 : (e + 1) * C // 16]),
+                COPY,
+            )
 
         def matmuls():
             for (g, e0, e1) in done_x:
@@ -156,16 +161,18 @@ def tile_routed_moe_kernel(tc, xT, w, b, gate, offs, pos1, pos2, out):
             done_x.append((g, e0, e1))
             matmuls()
 
-        def interleave_w(e):
-            for g in range(0, G, W_PIECE):
-                nc.gpsimd.tensor_scalar(
-                    wq[e][:, g : g + W_PIECE, :].rearrange("p g (n t) -> p g n t", t=4),
-                    wr[e][:, g : g + W_PIECE, :].rearrange("p g (t n) -> p g n t", t=4),
-                    1.0,
-                    0.0,
-                    MULT,
-                    ADD,
-                )
+        def quantize_unit(g, h):
+            quantize_x(g, 4 * h, 4 * h + 4, qt[V_UNITS.index((g, h))][:])
+
+        def interleave_w(piece):
+            nc.gpsimd.tensor_scalar(
+                wq[piece // G][:, piece % G, :].rearrange("p (n t) -> p n t", t=4),
+                wr[piece][:].rearrange("p (t n) -> p n t", t=4),
+                1.0,
+                0.0,
+                MULT,
+                ADD,
+            )
 
         def quantize_w(e):
             nc.vector.quantize_mx(
@@ -174,34 +181,38 @@ def tile_routed_moe_kernel(tc, xT, w, b, gate, offs, pos1, pos2, out):
             done_w.append(e)
             matmuls()
 
-        for e in range(3):
-            interleave_w(e)
-        for t in range(4):
-            nc.gpsimd.tensor_scalar(xb[2][:, t, :], xp[2][t][:, 0:T], 1.0, 0.0, MULT, ADD)
-        for e in range(3, E):
-            if e >= 5:
-                load_w(e)
-            interleave_w(e)
-
         for i in range(len(V_UNITS)):
             gather(i)
 
-        nc.scalar.copy(out=xb[3][:], in_=xraw[:])
-        for step in S_STEPS:
-            if step[0] == "f":
-                scalar_gather(step[1], step[2])
-            else:
-                interleave(step[1])
-        for i in V_INTERLEAVES:
-            interleave(i)
+        for piece in range(E * G):
+            if piece in G_BEFORE:
+                interleave(G_BEFORE[piece])
+            interleave_w(piece)
 
-        for i in range(len(V_UNITS)):
-            g, h = V_UNITS[i]
-            quantize_x(g, 4 * h, 4 * h + 4, qt[i][:])
+        for t in range(4):
+            nc.scalar.copy(out=xb[3][:, t, :], in_=xraw[:, t, :])
+            for e in range(E):
+                scalar_gather(3, t, e)
+
+        interleave(2)
+        interleave(4)
+        for g in range(3):
+            quantize_unit(g, 0)
         quantize_x(3, 0, 4, qs[(3, 0)][:].rearrange("p j t -> p (j t)"))
-        for e in range(E):
+        for e in range(4):
             quantize_w(e)
+
+        for t in range(4):
+            nc.scalar.copy(out=xb[2][:, t, :], in_=xp[2][t][:, 0:T])
+        for e in range(4, E):
+            for t in range(4):
+                scalar_gather(2, t, e)
+        interleave(3)
+        for g in range(2):
+            quantize_unit(g, 1)
         quantize_x(3, 4, 8, qs[(3, 1)][:].rearrange("p j t -> p (j t)"))
+        for e in range(4, E):
+            quantize_w(e)
         flat = qs[(2, 1)][:].rearrange("p j t -> p (j t)")
         quantize_x(2, 4, 6, flat[:, 0 : 8 * C])
         quantize_x(2, 6, 8, flat[:, 8 * C : 16 * C])

@@ -22,16 +22,10 @@ S = E * C
 HALF = 512
 PAD = 32
 
-V_UNITS = ((0, 0), (0, 1), (1, 0), (1, 1), (2, 0))
-V_INTERLEAVES = (3, 4)
-G_INTERLEAVES = (0, 1)
-X_LOADS = (
-    (0, 0, 0), (3, 0, 0), (0, 1, 0), (0, 2, 1), (0, 3, 2), (3, 1, 4), (3, 2, 10), (1, 0, 10),
-    (1, 1, 11), (1, 2, 12), (1, 3, 13), (3, 3, 13), (2, 0, 14), (2, 1, 15), (2, 2, 16), (2, 3, 17),
-)
-G_BEFORE = {5: 0, 9: 1}
-W_BUFS = 16
-GT_BUFS = 4
+V_UNITS = ((0, 0), (0, 1), (1, 0), (1, 1))
+V_INTERLEAVES = (0, 1, 2, 3)
+N_G = 4
+S_W = ()
 
 
 def tile_routed_moe_kernel(tc, xT, w, b, gate, offs, pos1, pos2, out):
@@ -46,15 +40,12 @@ def tile_routed_moe_kernel(tc, xT, w, b, gate, offs, pos1, pos2, out):
         pos1_t = lists.tile([P, T // 16], U16, name="pos1_t")
         pos2_t = lists.tile([P, T // 16], U16, name="pos2_t")
 
-        xp = [[keep.tile([P, T + PAD], F32, name="xp%d%d" % (g, t)) for t in range(4)] for g in range(3)]
-        xraw = keep.tile([P, 4, T], F32, name="xraw")
+        xp = [[keep.tile([P, T + PAD], F32, name="xp%d%d" % (g, t)) for t in range(4)] for g in range(2)]
+        xraw = {g: keep.tile([P, 4, T], F32, name="xraw%d" % g) for g in (2, 3)}
         xb = {g: keep.tile([P, 4, T], BF16, name="xb%d" % g) for g in (2, 3)}
-        qs = {
-            (g, h): keep.tile([P, HALF, 4], BF16, name="qs%d%d" % (g, h), align_bytes=64)
-            for (g, h) in ((3, 0), (3, 1), (2, 1))
-        }
+        qs = {g: keep.tile([P, S, 4], BF16, name="qs%d" % g, align_bytes=64) for g in (2, 3)}
         qt = [keep.tile([P, 4 * HALF], BF16, name="qt%d" % i, align_bytes=64) for i in range(len(V_UNITS))]
-        wq = [keep.tile([P, G, 4 * N], BF16, name="wq%d" % e, align_bytes=64) for e in range(E)]
+        wr = [keep.tile([P, G, 4 * N], F32, name="wr%d" % e) for e in range(E)]
         xc = keep.tile([P, G, S], U32, name="xc", align_bytes=64)
         xs = keep.tile([P, G, S], U8, name="xs", align_bytes=64)
         wc = keep.tile([P, E, G * N], U32, name="wc", align_bytes=64)
@@ -66,26 +57,35 @@ def tile_routed_moe_kernel(tc, xT, w, b, gate, offs, pos1, pos2, out):
         acc = [psum.tile([P, C], F32, name="acc%d" % e) for e in range(E)]
 
         xv = xT.rearrange("(g p t) n -> g p t n", p=P, t=4)
-        wv = w.rearrange("e (g p t) n -> e g p (t n)", p=P, t=4)
-        wr = {}
+        wv = w.rearrange("e (g p t) n -> e p g (t n)", p=P, t=4)
 
-        def load_w(piece):
-            wr[piece] = ring.tile([P, 4 * N], F32, name="wr", bufs=W_BUFS)
-            nc.sync.dma_start(out=wr[piece][:], in_=wv[piece // G, piece % G])
+        def load_planes(g, planes):
+            for t in planes:
+                nc.sync.dma_start(out=xp[g][t][:, 0:T], in_=xv[g, :, t, :])
+
+        def load_pass(g):
+            nc.sync.dma_start(out=xraw[g][:], in_=xv[g])
+
+        def load_pass_plane(g, t):
+            nc.sync.dma_start(out=xraw[g][:, t, :], in_=xv[g, :, t, :])
+
+        def load_w(e):
+            nc.sync.dma_start(out=wr[e][:], in_=wv[e])
 
         nc.sync.dma_start(offs_t[:], offs)
-        loaded = 0
-        for (g, t, before) in X_LOADS:
-            while loaded < before:
-                load_w(loaded)
-                loaded += 1
-            if g == 3:
-                nc.sync.dma_start(out=xraw[:, t, :], in_=xv[g, :, t, :])
-            else:
-                nc.sync.dma_start(out=xp[g][t][:, 0:T], in_=xv[g, :, t, :])
-        while loaded < E * G:
-            load_w(loaded)
-            loaded += 1
+        load_planes(0, (0,))
+        load_pass_plane(3, 0)
+        load_planes(0, (1, 2, 3))
+        load_w(0)
+        for t in range(1, 4):
+            load_pass_plane(3, t)
+        load_w(1)
+        load_planes(1, (0, 1, 2, 3))
+        load_w(2)
+        load_w(3)
+        load_pass(2)
+        for e in range(4, E):
+            load_w(e)
         nc.sync.dma_start(pos1_t[:], pos1)
         nc.sync.dma_start(pos2_t[:], pos2)
         nc.sync.dma_start(out=b_t[:], in_=b)
@@ -96,18 +96,19 @@ def tile_routed_moe_kernel(tc, xT, w, b, gate, offs, pos1, pos2, out):
         warm2 = keep.tile([P, 1], F32, name="warm2")
         nc.gpsimd.memset(warm[:], 0.0)
         nc.scalar.activation(out=warm2[:], in_=warm[:], func=GELU)
-        for g in range(3):
+        for g in range(2):
             for t in range(4):
                 nc.gpsimd.memset(xp[g][t][:, T : T + PAD], 0.0)
 
         gathered = {}
+        w_grouped = {}
         done_x = []
         done_w = []
         issued = {}
 
         def gather(i):
             g, h = V_UNITS[i]
-            gt = ring.tile([P, 4, HALF], F32, name="gt", bufs=GT_BUFS)
+            gt = ring.tile([P, 4, HALF], F32, name="gt", bufs=4)
             gathered[i] = gt
             col = h * HALF // 16
             for t in range(4):
@@ -118,18 +119,12 @@ def tile_routed_moe_kernel(tc, xT, w, b, gate, offs, pos1, pos2, out):
             src = gathered[i][:].rearrange("p t j -> p j t")
             if i in V_INTERLEAVES:
                 nc.vector.tensor_copy(out=dst, in_=src)
-            elif i in G_INTERLEAVES:
-                for c in range(4):
-                    nc.gpsimd.tensor_scalar(
-                        dst[:, c * C : (c + 1) * C, :], src[:, c * C : (c + 1) * C, :], 1.0, 0.0, MULT, ADD
-                    )
             else:
                 nc.scalar.copy(out=dst, in_=src)
 
         def scalar_gather(g, t, e):
-            h, c = divmod(e, 4)
             nc.scalar.activation(
-                qs[(g, h)][:, c * C : (c + 1) * C, t],
+                qs[g][:, e * C : (e + 1) * C, t],
                 xb[g][:, t, :].indirect(offs_t[:, e * C // 16 : (e + 1) * C // 16]),
                 COPY,
             )
@@ -161,61 +156,56 @@ def tile_routed_moe_kernel(tc, xT, w, b, gate, offs, pos1, pos2, out):
             done_x.append((g, e0, e1))
             matmuls()
 
-        def quantize_unit(g, h):
-            quantize_x(g, 4 * h, 4 * h + 4, qt[V_UNITS.index((g, h))][:])
+        def quantize_scalar_pass(g, e0, e1):
+            quantize_x(g, e0, e1, qs[g][:].rearrange("p j t -> p (j t)")[:, e0 * 4 * C : e1 * 4 * C])
 
-        def interleave_w(piece):
-            nc.gpsimd.tensor_scalar(
-                wq[piece // G][:, piece % G, :].rearrange("p (n t) -> p n t", t=4),
-                wr[piece][:].rearrange("p (t n) -> p n t", t=4),
-                1.0,
-                0.0,
-                MULT,
-                ADD,
-            )
+        def interleave_w(e):
+            wq = ring.tile([P, G, 4 * N], BF16, name="wq", align_bytes=64, bufs=4)
+            w_grouped[e] = wq
+            dst = wq[:].rearrange("p g (n t) -> p g n t", t=4)
+            src = wr[e][:].rearrange("p g (t n) -> p g n t", t=4)
+            if e < N_G:
+                nc.gpsimd.tensor_scalar(dst, src, 1.0, 0.0, MULT, ADD)
+            elif e in S_W:
+                nc.scalar.copy(out=dst, in_=src)
+            else:
+                nc.vector.tensor_copy(out=dst, in_=src)
 
         def quantize_w(e):
             nc.vector.quantize_mx(
-                out=wc[:, e, :].bitcast(FP8X4), scales=ws[:, e, :], in_=wq[e][:].rearrange("p g c -> p (g c)")
+                out=wc[:, e, :].bitcast(FP8X4), scales=ws[:, e, :], in_=w_grouped[e][:].rearrange("p g c -> p (g c)")
             )
             done_w.append(e)
             matmuls()
 
         for i in range(len(V_UNITS)):
             gather(i)
-
-        for piece in range(E * G):
-            if piece in G_BEFORE:
-                interleave(G_BEFORE[piece])
-            interleave_w(piece)
+        for e in range(N_G):
+            interleave_w(e)
 
         for t in range(4):
-            nc.scalar.copy(out=xb[3][:, t, :], in_=xraw[:, t, :])
+            nc.scalar.copy(out=xb[3][:, t, :], in_=xraw[3][:, t, :])
             for e in range(E):
                 scalar_gather(3, t, e)
+        for i in range(len(V_UNITS)):
+            interleave(i)
+        nc.scalar.copy(out=xb[2][:], in_=xraw[2][:])
 
-        interleave(2)
-        interleave(4)
-        for g in range(3):
-            quantize_unit(g, 0)
-        quantize_x(3, 0, 4, qs[(3, 0)][:].rearrange("p j t -> p (j t)"))
-        for e in range(4):
+        for e in range(E):
+            if e >= N_G:
+                interleave_w(e)
             quantize_w(e)
+        for i in range(len(V_UNITS)):
+            g, h = V_UNITS[i]
+            quantize_x(g, 4 * h, 4 * h + 4, qt[i][:])
+        quantize_scalar_pass(3, 0, 4)
+        quantize_scalar_pass(3, 4, 8)
 
-        for t in range(4):
-            nc.scalar.copy(out=xb[2][:, t, :], in_=xp[2][t][:, 0:T])
-        for e in range(4, E):
-            for t in range(4):
-                scalar_gather(2, t, e)
-        interleave(3)
-        for g in range(2):
-            quantize_unit(g, 1)
-        quantize_x(3, 4, 8, qs[(3, 1)][:].rearrange("p j t -> p (j t)"))
-        for e in range(4, E):
-            quantize_w(e)
-        flat = qs[(2, 1)][:].rearrange("p j t -> p (j t)")
-        quantize_x(2, 4, 6, flat[:, 0 : 8 * C])
-        quantize_x(2, 6, 8, flat[:, 8 * C : 16 * C])
+        for e0 in range(0, E, 2):
+            for e in (e0, e0 + 1):
+                for t in range(4):
+                    scalar_gather(2, t, e)
+            quantize_scalar_pass(2, e0, e0 + 2)
 
         t1 = keep.tile([P, T], F32, name="t1")
         t2 = keep.tile([P, T], F32, name="t2")

@@ -40,16 +40,16 @@ def tile_routed_moe_kernel(tc, xT, w, b, gate, offs, pos1, pos2, out):
         pos1_t = lists.tile([P, T // 16], U16, name="pos1_t")
         pos2_t = lists.tile([P, T // 16], U16, name="pos2_t")
 
-        xp = [[keep.tile([P, T + PAD], F32, name="xp%d%d" % (g, t)) for t in range(4)] for g in range(2)]
+        xp = [
+            [keep.tile([P, T + PAD], F32, name="xp%d%d" % (g, t), tag="win%d%d" % (g, t), align_bytes=64) for t in range(4)]
+            for g in range(2)
+        ]
         xraw = {g: keep.tile([P, 4, T], F32, name="xraw%d" % g) for g in (2, 3)}
         xb = {g: keep.tile([P, 4, T], BF16, name="xb%d" % g) for g in (2, 3)}
         qs = {g: keep.tile([P, S, 4], BF16, name="qs%d" % g, align_bytes=64) for g in (2, 3)}
-        qt = [keep.tile([P, 4 * HALF], BF16, name="qt%d" % i, align_bytes=64) for i in range(len(V_UNITS))]
         wr = [keep.tile([P, G, 4 * N], F32, name="wr%d" % e) for e in range(E)]
         xc = keep.tile([P, G, S], U32, name="xc", align_bytes=64)
-        xs = keep.tile([P, G, S], U8, name="xs", align_bytes=64)
         wc = keep.tile([P, E, G * N], U32, name="wc", align_bytes=64)
-        ws = keep.tile([P, E, G * N], U8, name="ws", align_bytes=64)
         b_t = keep.tile([P, E], F32, name="b_t")
         gate0 = keep.tile([P, T], F32, name="gate0")
         gate1 = keep.tile([P, T], F32, name="gate1")
@@ -180,6 +180,11 @@ def tile_routed_moe_kernel(tc, xT, w, b, gate, offs, pos1, pos2, out):
 
         for i in range(len(V_UNITS)):
             gather(i)
+        scales = keep.tile([P, 2 * G * S], U8, name="scales", tag="win13", align_bytes=64)
+        qt = [keep.tile([P, 4 * HALF], BF16, name="qt%d" % i, tag="win1%d" % (2 - i), align_bytes=64) for i in range(3)]
+        qt.append(keep.tile([P, 4 * HALF], BF16, name="qt3", align_bytes=64))
+        xs = scales[:, 0 : G * S].rearrange("p (g s) -> p g s", g=G)
+        ws = scales[:, G * S : 2 * G * S].rearrange("p (e c) -> p e c", e=E)
         for e in range(N_G):
             interleave_w(e)
 

@@ -23,7 +23,7 @@ HALF = 512
 PAD = 32
 
 V_UNITS = ((0, 0), (0, 1), (1, 0), (1, 1))
-V_INTERLEAVES = (0, 1, 2, 3)
+G_INTERLEAVES = (0, 1)
 N_G = 4
 S_W = ()
 
@@ -45,7 +45,7 @@ def tile_routed_moe_kernel(tc, xT, w, b, gate, offs, pos1, pos2, out):
             for g in range(2)
         ]
         xraw = {g: keep.tile([P, 4, T], F32, name="xraw%d" % g) for g in (2, 3)}
-        xb = {g: keep.tile([P, 4, T], BF16, name="xb%d" % g) for g in (2, 3)}
+        xb = {g: keep.tile([P, 4, T], BF16, name="xb%d" % g, tag="xb%d" % g) for g in (2, 3)}
         qs = {g: keep.tile([P, S, 4], BF16, name="qs%d" % g, align_bytes=64) for g in (2, 3)}
         wr = [keep.tile([P, G, 4 * N], F32, name="wr%d" % e) for e in range(E)]
         xc = keep.tile([P, G, S], U32, name="xc", align_bytes=64)
@@ -53,7 +53,6 @@ def tile_routed_moe_kernel(tc, xT, w, b, gate, offs, pos1, pos2, out):
         b_t = keep.tile([P, E], F32, name="b_t")
         gate0 = keep.tile([P, T], F32, name="gate0")
         gate1 = keep.tile([P, T], F32, name="gate1")
-        y = keep.tile([P, S], F32, name="y")
         acc = [psum.tile([P, C], F32, name="acc%d" % e) for e in range(E)]
 
         xv = xT.rearrange("(g p t) n -> g p t n", p=P, t=4)
@@ -75,13 +74,17 @@ def tile_routed_moe_kernel(tc, xT, w, b, gate, offs, pos1, pos2, out):
         nc.sync.dma_start(offs_t[:], offs)
         load_planes(0, (0,))
         load_pass_plane(3, 0)
-        load_planes(0, (1, 2, 3))
+        load_planes(0, (1,))
         load_w(0)
-        for t in range(1, 4):
-            load_pass_plane(3, t)
+        load_planes(0, (2,))
+        load_pass_plane(3, 1)
         load_w(1)
-        load_planes(1, (0, 1, 2, 3))
+        load_planes(0, (3,))
+        load_pass_plane(3, 2)
+        load_planes(1, (0, 1))
         load_w(2)
+        load_pass_plane(3, 3)
+        load_planes(1, (2, 3))
         load_w(3)
         load_pass(2)
         for e in range(4, E):
@@ -106,21 +109,18 @@ def tile_routed_moe_kernel(tc, xT, w, b, gate, offs, pos1, pos2, out):
         done_w = []
         issued = {}
 
-        def gather(i):
+        def gather(i, t):
             g, h = V_UNITS[i]
-            gt = ring.tile([P, 4, HALF], F32, name="gt", bufs=4)
-            gathered[i] = gt
             col = h * HALF // 16
-            for t in range(4):
-                nc.vector.tensor_copy(gt[:, t, :], xp[g][t][:].indirect(offs_t[:, col : col + HALF // 16]))
+            nc.vector.tensor_copy(gathered[i][:, t, :], xp[g][t][:].indirect(offs_t[:, col : col + HALF // 16]))
 
         def interleave(i):
             dst = qt[i][:].rearrange("p (j t) -> p j t", t=4)
             src = gathered[i][:].rearrange("p t j -> p j t")
-            if i in V_INTERLEAVES:
-                nc.vector.tensor_copy(out=dst, in_=src)
+            if i in G_INTERLEAVES:
+                nc.gpsimd.tensor_scalar(dst, src, 1.0, 0.0, MULT, ADD)
             else:
-                nc.scalar.copy(out=dst, in_=src)
+                nc.vector.tensor_copy(out=dst, in_=src)
 
         def scalar_gather(g, t, e):
             nc.scalar.activation(
@@ -160,7 +160,10 @@ def tile_routed_moe_kernel(tc, xT, w, b, gate, offs, pos1, pos2, out):
             quantize_x(g, e0, e1, qs[g][:].rearrange("p j t -> p (j t)")[:, e0 * 4 * C : e1 * 4 * C])
 
         def interleave_w(e):
-            wq = ring.tile([P, G, 4 * N], BF16, name="wq", align_bytes=64, bufs=4)
+            if e < N_G or e in S_W:
+                wq = keep.tile([P, G, 4 * N], BF16, name="wq%d" % e, align_bytes=64)
+            else:
+                wq = keep.tile([P, G, 4 * N], BF16, name="wq%d" % e, tag="win1%d" % (e % 2), align_bytes=64)
             w_grouped[e] = wq
             dst = wq[:].rearrange("p g (n t) -> p g n t", t=4)
             src = wr[e][:].rearrange("p g (t n) -> p g n t", t=4)
@@ -179,26 +182,38 @@ def tile_routed_moe_kernel(tc, xT, w, b, gate, offs, pos1, pos2, out):
             matmuls()
 
         for i in range(len(V_UNITS)):
-            gather(i)
+            gathered[i] = ring.tile([P, 4, HALF], F32, name="gt%d" % i, tag="gt", bufs=4)
+        for g in range(2):
+            for t in range(4):
+                for h in range(2):
+                    gather(2 * g + h, t)
         scales = keep.tile([P, 2 * G * S], U8, name="scales", tag="win13", align_bytes=64)
-        qt = [keep.tile([P, 4 * HALF], BF16, name="qt%d" % i, tag="win1%d" % (2 - i), align_bytes=64) for i in range(3)]
+        qt = [keep.tile([P, 4 * HALF], BF16, name="qt%d" % i, align_bytes=64) for i in (0, 1)]
+        qt.append(keep.tile([P, 4 * HALF], BF16, name="qt2", tag="win12", align_bytes=64))
         qt.append(keep.tile([P, 4 * HALF], BF16, name="qt3", align_bytes=64))
         xs = scales[:, 0 : G * S].rearrange("p (g s) -> p g s", g=G)
         ws = scales[:, G * S : 2 * G * S].rearrange("p (e c) -> p e c", e=E)
-        for e in range(N_G):
-            interleave_w(e)
+        interleave_w(0)
+        interleave_w(1)
+        interleave(0)
+        interleave(1)
+        interleave_w(2)
+        interleave_w(3)
 
         for t in range(4):
             nc.scalar.copy(out=xb[3][:, t, :], in_=xraw[3][:, t, :])
             for e in range(E):
                 scalar_gather(3, t, e)
-        for i in range(len(V_UNITS)):
+        for i in (2, 3):
             interleave(i)
         nc.scalar.copy(out=xb[2][:], in_=xraw[2][:])
 
-        for e in range(E):
-            if e >= N_G:
-                interleave_w(e)
+        for e in range(N_G):
+            quantize_w(e)
+        interleave_w(N_G)
+        for e in range(N_G, E):
+            if e + 1 < E:
+                interleave_w(e + 1)
             quantize_w(e)
         for i in range(len(V_UNITS)):
             g, h = V_UNITS[i]
@@ -206,15 +221,18 @@ def tile_routed_moe_kernel(tc, xT, w, b, gate, offs, pos1, pos2, out):
         quantize_scalar_pass(3, 0, 4)
         quantize_scalar_pass(3, 4, 8)
 
-        for e0 in range(0, E, 2):
-            for e in (e0, e0 + 1):
-                for t in range(4):
-                    scalar_gather(2, t, e)
+        for e in range(E):
+            for t in range(4):
+                scalar_gather(2, t, e)
+        y = keep.tile([P, S], F32, name="y", tag="xb2")
+        for e0 in range(0, E - 2, 2):
             quantize_scalar_pass(2, e0, e0 + 2)
+        quantize_scalar_pass(2, E - 2, E - 1)
+        quantize_scalar_pass(2, E - 1, E)
 
-        t1 = keep.tile([P, T], F32, name="t1")
-        t2 = keep.tile([P, T], F32, name="t2")
-        res = keep.tile([P, T], F32, name="res")
+        t1 = ring.tile([P, T], F32, name="t1", tag="gt", bufs=4)
+        t2 = ring.tile([P, T], F32, name="t2", tag="gt", bufs=4)
+        res = ring.tile([P, T], F32, name="res", tag="gt", bufs=4)
         nc.vector.tensor_tensor(t1[:], y[:].indirect(pos1_t[:]), gate0[:], MULT)
         nc.vector.tensor_tensor(t2[:], y[:].indirect(pos2_t[:]), gate1[:], MULT)
         nc.vector.tensor_tensor(res[:], t1[:], t2[:], ADD)

@@ -24,7 +24,7 @@ PAD = 32
 
 V_UNITS = ((0, 0), (0, 1), (1, 0), (1, 1))
 G_INTERLEAVES = (0, 1)
-N_G = 4
+N_G = 3
 S_W = ()
 
 
@@ -82,12 +82,10 @@ def tile_routed_moe_kernel(tc, xT, w, b, gate, offs, pos1, pos2, out):
         load_planes(0, (3,))
         load_pass_plane(3, 2)
         load_planes(1, (0, 1))
-        load_w(2)
+        load_pass(2)
         load_pass_plane(3, 3)
         load_planes(1, (2, 3))
-        load_w(3)
-        load_pass(2)
-        for e in range(4, E):
+        for e in range(2, E):
             load_w(e)
         nc.sync.dma_start(pos1_t[:], pos1)
         nc.sync.dma_start(pos2_t[:], pos2)
@@ -196,9 +194,9 @@ def tile_routed_moe_kernel(tc, xT, w, b, gate, offs, pos1, pos2, out):
         interleave_w(0)
         interleave_w(1)
         interleave(0)
+        nc.gpsimd.tensor_scalar(xb[2][:], xraw[2][:], 1.0, 0.0, MULT, ADD)
         interleave(1)
         interleave_w(2)
-        interleave_w(3)
 
         for t in range(4):
             nc.scalar.copy(out=xb[3][:, t, :], in_=xraw[3][:, t, :])
@@ -206,7 +204,6 @@ def tile_routed_moe_kernel(tc, xT, w, b, gate, offs, pos1, pos2, out):
                 scalar_gather(3, t, e)
         for i in (2, 3):
             interleave(i)
-        nc.scalar.copy(out=xb[2][:], in_=xraw[2][:])
 
         for e in range(N_G):
             quantize_w(e)

@@ -113,11 +113,13 @@ def tile_routed_moe_kernel(tc, xT, w, b, gate, offs, pos1, pos2, out):
             nc.vector.tensor_copy(gathered[i][:, t, :], xp[g][t][:].indirect(offs_t[:, col : col + HALF // 16]))
 
         def interleave(i):
-            dst = qt[i][:].rearrange("p (j t) -> p j t", t=4)
-            src = gathered[i][:].rearrange("p t j -> p j t")
             if i in G_INTERLEAVES:
+                dst = qt[i][:].rearrange("p (j t) -> p j t", t=4)
+                src = gathered[i][:].rearrange("p t j -> p j t")
                 nc.gpsimd.tensor_scalar(dst, src, 1.0, 0.0, MULT, ADD)
             else:
+                dst = qt[i][:].rearrange("p (c i t) -> p c t i", i=4, t=4)
+                src = gathered[i][:].rearrange("p t (c i) -> p c t i", i=4)
                 nc.vector.tensor_copy(out=dst, in_=src)
 
         def scalar_gather(g, t, e):
@@ -170,6 +172,8 @@ def tile_routed_moe_kernel(tc, xT, w, b, gate, offs, pos1, pos2, out):
             elif e in S_W:
                 nc.scalar.copy(out=dst, in_=src)
             else:
+                dst = wq[:].rearrange("p g (c i t) -> p g c t i", i=4, t=4)
+                src = wr[e][:].rearrange("p g (t c i) -> p g c t i", t=4, i=4)
                 nc.vector.tensor_copy(out=dst, in_=src)
 
         def quantize_w(e):

@@ -24,7 +24,7 @@ PAD = 32
 
 V_UNITS = ((0, 0), (0, 1), (1, 0), (1, 1))
 G_INTERLEAVES = (0, 1)
-N_G = 3
+N_G = 2
 S_W = ()
 
 
@@ -200,7 +200,6 @@ def tile_routed_moe_kernel(tc, xT, w, b, gate, offs, pos1, pos2, out):
         interleave(0)
         nc.gpsimd.tensor_scalar(xb[2][:], xraw[2][:], 1.0, 0.0, MULT, ADD)
         interleave(1)
-        interleave_w(2)
 
         for t in range(4):
             nc.scalar.copy(out=xb[3][:, t, :], in_=xraw[3][:, t, :])

@@ -25,7 +25,7 @@ PAD = 32
 V_UNITS = ((0, 0), (0, 1), (1, 0), (1, 1))
 G_INTERLEAVES = (0, 1)
 N_G = 2
-S_W = ()
+S_W = (2,)
 
 
 def tile_routed_moe_kernel(tc, xT, w, b, gate, offs, pos1, pos2, out):
@@ -170,7 +170,11 @@ def tile_routed_moe_kernel(tc, xT, w, b, gate, offs, pos1, pos2, out):
             if e < N_G:
                 nc.gpsimd.tensor_scalar(dst, src, 1.0, 0.0, MULT, ADD)
             elif e in S_W:
-                nc.scalar.copy(out=dst, in_=src)
+                for g in range(G):
+                    nc.scalar.copy(
+                        out=wq[:, g, :].rearrange("p (c i t) -> p c t i", i=4, t=4),
+                        in_=wr[e][:, g, :].rearrange("p (t c i) -> p c t i", t=4, i=4),
+                    )
             else:
                 dst = wq[:].rearrange("p g (c i t) -> p g c t i", i=4, t=4)
                 src = wr[e][:].rearrange("p g (t c i) -> p g c t i", t=4, i=4)

@@ -71,20 +71,27 @@ def tile_routed_moe_kernel(tc, xT, w, b, gate, offs, pos1, pos2, out):
         def load_w(e):
             nc.sync.dma_start(out=wr[e][:], in_=wv[e])
 
+        def load_w_half(e, u):
+            nc.sync.dma_start(out=wr[e][:, 2 * u : 2 * u + 2, :], in_=wv[e][:, 2 * u : 2 * u + 2, :])
+
         nc.sync.dma_start(offs_t[:], offs)
         load_planes(0, (0,))
         load_pass_plane(3, 0)
         load_planes(0, (1,))
-        load_w(0)
+        load_w_half(0, 0)
+        load_w_half(0, 1)
         load_planes(0, (2,))
         load_pass_plane(3, 1)
-        load_w(1)
         load_planes(0, (3,))
+        load_w_half(1, 0)
+        load_w_half(1, 1)
+        load_planes(1, (0,))
         load_pass_plane(3, 2)
-        load_planes(1, (0, 1))
+        load_planes(1, (1,))
         load_pass(2)
+        load_planes(1, (2,))
         load_pass_plane(3, 3)
-        load_planes(1, (2, 3))
+        load_planes(1, (3,))
         for e in range(2, E):
             load_w(e)
         nc.sync.dma_start(pos1_t[:], pos1)
@@ -168,7 +175,8 @@ def tile_routed_moe_kernel(tc, xT, w, b, gate, offs, pos1, pos2, out):
             dst = wq[:].rearrange("p g (n t) -> p g n t", t=4)
             src = wr[e][:].rearrange("p g (t n) -> p g n t", t=4)
             if e < N_G:
-                nc.gpsimd.tensor_scalar(dst, src, 1.0, 0.0, MULT, ADD)
+                for u in range(2):
+                    nc.gpsimd.tensor_scalar(dst[:, 2 * u : 2 * u + 2], src[:, 2 * u : 2 * u + 2], 1.0, 0.0, MULT, ADD)
             elif e in S_W:
                 for g in range(G):
                     nc.scalar.copy(

@@ -223,15 +223,15 @@ def tile_routed_moe_kernel(tc, xT, w, b, gate, offs, pos1, pos2, out):
         for e in range(N_G):
             quantize_w(e)
         interleave_w(N_G)
-        for e in range(N_G, E):
-            if e + 1 < E:
-                interleave_w(e + 1)
-            quantize_w(e)
         for i in range(len(V_UNITS)):
             g, h = V_UNITS[i]
             quantize_x(g, 4 * h, 4 * h + 4, qt[i][:])
         quantize_scalar_pass(3, 0, 4)
         quantize_scalar_pass(3, 4, 8)
+        for e in range(N_G, E):
+            if e + 1 < E:
+                interleave_w(e + 1)
+            quantize_w(e)
 
         for e in range(E):
             for t in range(4):

@@ -78,10 +78,10 @@ def tile_routed_moe_kernel(tc, xT, w, b, gate, offs, pos1, pos2, out):
         load_planes(0, (0,))
         load_pass_plane(3, 0)
         load_planes(0, (1,))
-        load_w_half(0, 0)
-        load_w_half(0, 1)
-        load_planes(0, (2,))
         load_pass_plane(3, 1)
+        load_w_half(0, 0)
+        load_planes(0, (2,))
+        load_w_half(0, 1)
         load_planes(0, (3,))
         load_w_half(1, 0)
         load_w_half(1, 1)
@@ -178,11 +178,23 @@ def tile_routed_moe_kernel(tc, xT, w, b, gate, offs, pos1, pos2, out):
                 for u in range(2):
                     nc.gpsimd.tensor_scalar(dst[:, 2 * u : 2 * u + 2], src[:, 2 * u : 2 * u + 2], 1.0, 0.0, MULT, ADD)
             elif e in S_W:
-                for g in range(G):
-                    nc.scalar.copy(
-                        out=wq[:, g, :].rearrange("p (c i t) -> p c t i", i=4, t=4),
-                        in_=wr[e][:, g, :].rearrange("p (t c i) -> p c t i", t=4, i=4),
-                    )
+                nc.scalar.copy(
+                    out=wq[:].rearrange("p g (c i t) -> p g c t i", i=4, t=4),
+                    in_=wr[e][:].rearrange("p g (t c i) -> p g c t i", t=4, i=4),
+                )
+            elif e == 3:
+                nc.scalar.copy(
+                    out=wq[:, 0, :].rearrange("p (c i t) -> p c t i", i=4, t=4),
+                    in_=wr[e][:, 0, :].rearrange("p (t c i) -> p c t i", t=4, i=4),
+                )
+                nc.vector.tensor_copy(
+                    out=wq[:, 1, :].rearrange("p (c i t) -> p c t i", i=4, t=4),
+                    in_=wr[e][:, 1, :].rearrange("p (t c i) -> p c t i", t=4, i=4),
+                )
+                nc.vector.tensor_copy(
+                    out=wq[:, 2:G, :].rearrange("p g (c i t) -> p g c t i", i=4, t=4),
+                    in_=wr[e][:, 2:G, :].rearrange("p g (t c i) -> p g c t i", t=4, i=4),
+                )
             else:
                 dst = wq[:].rearrange("p g (c i t) -> p g c t i", i=4, t=4)
                 src = wr[e][:].rearrange("p g (t c i) -> p g c t i", t=4, i=4)
@@ -207,6 +219,7 @@ def tile_routed_moe_kernel(tc, xT, w, b, gate, offs, pos1, pos2, out):
         qt.append(keep.tile([P, 4 * HALF], BF16, name="qt3", align_bytes=64))
         xs = scales[:, 0 : G * S].rearrange("p (g s) -> p g s", g=G)
         ws = scales[:, G * S : 2 * G * S].rearrange("p (e c) -> p e c", e=E)
+        nc.gpsimd.tensor_scalar(xb[3][:, 1, :], xraw[3][:, 1, :], 1.0, 0.0, MULT, ADD)
         interleave_w(0)
         interleave_w(1)
         interleave(0)
@@ -214,7 +227,8 @@ def tile_routed_moe_kernel(tc, xT, w, b, gate, offs, pos1, pos2, out):
         interleave(1)
 
         for t in range(4):
-            nc.scalar.copy(out=xb[3][:, t, :], in_=xraw[3][:, t, :])
+            if t != 1:
+                nc.scalar.copy(out=xb[3][:, t, :], in_=xraw[3][:, t, :])
             for e in range(E):
                 scalar_gather(3, t, e)
         for i in (2, 3):
@@ -247,5 +261,7 @@ def tile_routed_moe_kernel(tc, xT, w, b, gate, offs, pos1, pos2, out):
         res = ring.tile([P, T], F32, name="res", tag="gt", bufs=4)
         nc.vector.tensor_tensor(t1[:], y[:].indirect(pos1_t[:]), gate0[:], MULT)
         nc.vector.tensor_tensor(t2[:], y[:].indirect(pos2_t[:]), gate1[:], MULT)
-        nc.vector.tensor_tensor(res[:], t1[:], t2[:], ADD)
-        nc.sync.dma_start(out=out, in_=res[:])
+        for c0 in (0, T // 2):
+            cols = slice(c0, c0 + T // 2)
+            nc.vector.tensor_tensor(res[:, cols], t1[:, cols], t2[:, cols], ADD)
+            nc.sync.dma_start(out=out[:, cols], in_=res[:, cols])

@@ -170,7 +170,7 @@ def tile_routed_moe_kernel(tc, xT, w, b, gate, offs, pos1, pos2, out):
             if e < N_G or e in S_W:
                 wq = keep.tile([P, G, 4 * N], BF16, name="wq%d" % e, align_bytes=64)
             else:
-                wq = keep.tile([P, G, 4 * N], BF16, name="wq%d" % e, tag="win1%d" % (e % 2), align_bytes=64)
+                wq = keep.tile([P, G, 4 * N], BF16, name="wq%d" % e, tag=("win10", "win11", "wq_third")[e % 3], align_bytes=64)
             w_grouped[e] = wq
             dst = wq[:].rearrange("p g (n t) -> p g n t", t=4)
             src = wr[e][:].rearrange("p g (t n) -> p g n t", t=4)
@@ -181,19 +181,6 @@ def tile_routed_moe_kernel(tc, xT, w, b, gate, offs, pos1, pos2, out):
                 nc.scalar.copy(
                     out=wq[:].rearrange("p g (c i t) -> p g c t i", i=4, t=4),
                     in_=wr[e][:].rearrange("p g (t c i) -> p g c t i", t=4, i=4),
-                )
-            elif e == 3:
-                nc.scalar.copy(
-                    out=wq[:, 0, :].rearrange("p (c i t) -> p c t i", i=4, t=4),
-                    in_=wr[e][:, 0, :].rearrange("p (t c i) -> p c t i", t=4, i=4),
-                )
-                nc.vector.tensor_copy(
-                    out=wq[:, 1, :].rearrange("p (c i t) -> p c t i", i=4, t=4),
-                    in_=wr[e][:, 1, :].rearrange("p (t c i) -> p c t i", t=4, i=4),
-                )
-                nc.vector.tensor_copy(
-                    out=wq[:, 2:G, :].rearrange("p g (c i t) -> p g c t i", i=4, t=4),
-                    in_=wr[e][:, 2:G, :].rearrange("p g (t c i) -> p g c t i", t=4, i=4),
                 )
             else:
                 dst = wq[:].rearrange("p g (c i t) -> p g c t i", i=4, t=4)
@@ -260,7 +247,11 @@ def tile_routed_moe_kernel(tc, xT, w, b, gate, offs, pos1, pos2, out):
         t2 = ring.tile([P, T], F32, name="t2", tag="gt", bufs=4)
         res = ring.tile([P, T], F32, name="res", tag="gt", bufs=4)
         nc.vector.tensor_tensor(t1[:], y[:].indirect(pos1_t[:]), gate0[:], MULT)
-        nc.vector.tensor_tensor(t2[:], y[:].indirect(pos2_t[:]), gate1[:], MULT)
+        for c0 in (0, T // 2):
+            cols = slice(c0, c0 + T // 2)
+            nc.vector.tensor_tensor(
+                t2[:, cols], y[:].indirect(pos2_t[:, c0 // 16 : (c0 + T // 2) // 16]), gate1[:, cols], MULT
+            )
         for c0 in (0, T // 2):
             cols = slice(c0, c0 + T // 2)
             nc.vector.tensor_tensor(res[:, cols], t1[:, cols], t2[:, cols], ADD)

@@ -56,11 +56,14 @@ def tile_routed_moe_kernel(tc, xT, w, b, gate, offs, pos1, pos2, out):
         acc = [psum.tile([P, C], F32, name="acc%d" % e) for e in range(E)]
 
         xv = xT.rearrange("(g p t) n -> g p t n", p=P, t=4)
+        xflat = xT.rearrange("k n -> (k n)")
         wv = w.rearrange("e (g p t) n -> e p g (t n)", p=P, t=4)
 
         def load_planes(g, planes):
             for t in planes:
-                nc.sync.dma_start(out=xp[g][t][:, 0:T], in_=xv[g, :, t, :])
+                first = (512 * g + t) * T
+                rows = xflat[first : first + P * 4 * T].rearrange("(p r) -> p r", r=4 * T)
+                nc.sync.dma_start(out=xp[g][t][:], in_=rows[:, 0 : T + PAD])
 
         def load_pass(g):
             nc.sync.dma_start(out=xraw[g][:], in_=xv[g])
@@ -104,9 +107,6 @@ def tile_routed_moe_kernel(tc, xT, w, b, gate, offs, pos1, pos2, out):
         warm2 = keep.tile([P, 1], F32, name="warm2")
         nc.gpsimd.memset(warm[:], 0.0)
         nc.scalar.activation(out=warm2[:], in_=warm[:], func=GELU)
-        for g in range(2):
-            for t in range(4):
-                nc.gpsimd.memset(xp[g][t][:, T : T + PAD], 0.0)
 
         gathered = {}
         w_grouped = {}
@@ -121,11 +121,11 @@ def tile_routed_moe_kernel(tc, xT, w, b, gate, offs, pos1, pos2, out):
 
         def interleave(i):
             if i in G_INTERLEAVES:
-                dst = qt[i][:].rearrange("p (j t) -> p j t", t=4)
+                dst = qt[i].rearrange("p (j t) -> p j t", t=4)
                 src = gathered[i][:].rearrange("p t j -> p j t")
                 nc.gpsimd.tensor_scalar(dst, src, 1.0, 0.0, MULT, ADD)
             else:
-                dst = qt[i][:].rearrange("p (c i t) -> p c t i", i=4, t=4)
+                dst = qt[i].rearrange("p (c i t) -> p c t i", i=4, t=4)
                 src = gathered[i][:].rearrange("p t (c i) -> p c t i", i=4)
                 nc.vector.tensor_copy(out=dst, in_=src)
 
@@ -167,31 +167,42 @@ def tile_routed_moe_kernel(tc, xT, w, b, gate, offs, pos1, pos2, out):
             quantize_x(g, e0, e1, qs[g][:].rearrange("p j t -> p (j t)")[:, e0 * 4 * C : e1 * 4 * C])
 
         def interleave_w(e):
-            if e < N_G or e in S_W:
-                wq = keep.tile([P, G, 4 * N], BF16, name="wq%d" % e, align_bytes=64)
+            if e < N_G:
+                wq = wq_g[:, e, :, :]
+            elif e in S_W:
+                wq = keep.tile([P, G, 4 * N], BF16, name="wq%d" % e, align_bytes=64)[:]
             else:
-                wq = keep.tile([P, G, 4 * N], BF16, name="wq%d" % e, tag=("win10", "win11", "wq_third")[e % 3], align_bytes=64)
+                wq = keep.tile([P, G, 4 * N], BF16, name="wq%d" % e, tag=("win10", "win11", "wq_third")[e % 3], align_bytes=64)[:]
             w_grouped[e] = wq
-            dst = wq[:].rearrange("p g (n t) -> p g n t", t=4)
+            dst = wq.rearrange("p g (n t) -> p g n t", t=4)
             src = wr[e][:].rearrange("p g (t n) -> p g n t", t=4)
             if e < N_G:
                 for u in range(2):
                     nc.gpsimd.tensor_scalar(dst[:, 2 * u : 2 * u + 2], src[:, 2 * u : 2 * u + 2], 1.0, 0.0, MULT, ADD)
             elif e in S_W:
                 nc.scalar.copy(
-                    out=wq[:].rearrange("p g (c i t) -> p g c t i", i=4, t=4),
+                    out=wq.rearrange("p g (c i t) -> p g c t i", i=4, t=4),
                     in_=wr[e][:].rearrange("p g (t c i) -> p g c t i", t=4, i=4),
                 )
             else:
-                dst = wq[:].rearrange("p g (c i t) -> p g c t i", i=4, t=4)
+                dst = wq.rearrange("p g (c i t) -> p g c t i", i=4, t=4)
                 src = wr[e][:].rearrange("p g (t c i) -> p g c t i", t=4, i=4)
                 nc.vector.tensor_copy(out=dst, in_=src)
 
         def quantize_w(e):
             nc.vector.quantize_mx(
-                out=wc[:, e, :].bitcast(FP8X4), scales=ws[:, e, :], in_=w_grouped[e][:].rearrange("p g c -> p (g c)")
+                out=wc[:, e, :].bitcast(FP8X4), scales=ws[:, e, :], in_=w_grouped[e].rearrange("p g c -> p (g c)")
             )
             done_w.append(e)
+            matmuls()
+
+        def quantize_w_gpsimd():
+            nc.vector.quantize_mx(
+                out=wc[:, 0:N_G, :].rearrange("p e c -> p (e c)").bitcast(FP8X4),
+                scales=ws[:, 0:N_G, :].rearrange("p e c -> p (e c)"),
+                in_=wq_g[:].rearrange("p e g c -> p (e g c)"),
+            )
+            done_w.extend(range(N_G))
             matmuls()
 
         for i in range(len(V_UNITS)):
@@ -201,9 +212,11 @@ def tile_routed_moe_kernel(tc, xT, w, b, gate, offs, pos1, pos2, out):
                 for h in range(2):
                     gather(2 * g + h, t)
         scales = keep.tile([P, 2 * G * S], U8, name="scales", tag="win13", align_bytes=64)
-        qt = [keep.tile([P, 4 * HALF], BF16, name="qt%d" % i, align_bytes=64) for i in (0, 1)]
-        qt.append(keep.tile([P, 4 * HALF], BF16, name="qt2", tag="win12", align_bytes=64))
-        qt.append(keep.tile([P, 4 * HALF], BF16, name="qt3", align_bytes=64))
+        qt_g = keep.tile([P, 2 * 4 * HALF], BF16, name="qt_g", align_bytes=64)
+        qt2 = keep.tile([P, 4 * HALF], BF16, name="qt2", tag="win12", align_bytes=64)
+        qt3 = keep.tile([P, 4 * HALF], BF16, name="qt3", align_bytes=64)
+        qt = [qt_g[:, 0 : 4 * HALF], qt_g[:, 4 * HALF : 2 * 4 * HALF], qt2[:], qt3[:]]
+        wq_g = keep.tile([P, N_G, G, 4 * N], BF16, name="wq_g", align_bytes=64)
         xs = scales[:, 0 : G * S].rearrange("p (g s) -> p g s", g=G)
         ws = scales[:, G * S : 2 * G * S].rearrange("p (e c) -> p e c", e=E)
         nc.gpsimd.tensor_scalar(xb[3][:, 1, :], xraw[3][:, 1, :], 1.0, 0.0, MULT, ADD)
@@ -221,14 +234,12 @@ def tile_routed_moe_kernel(tc, xT, w, b, gate, offs, pos1, pos2, out):
         for i in (2, 3):
             interleave(i)
 
-        for e in range(N_G):
-            quantize_w(e)
+        quantize_w_gpsimd()
         interleave_w(N_G)
-        for i in range(len(V_UNITS)):
-            g, h = V_UNITS[i]
-            quantize_x(g, 4 * h, 4 * h + 4, qt[i][:])
-        quantize_scalar_pass(3, 0, 4)
-        quantize_scalar_pass(3, 4, 8)
+        quantize_x(0, 0, E, qt_g[:])
+        quantize_x(1, 0, 4, qt[2])
+        quantize_x(1, 4, E, qt[3])
+        quantize_scalar_pass(3, 0, E)
         for e in range(N_G, E):
             if e + 1 < E:
                 interleave_w(e + 1)

@@ -25,7 +25,7 @@ PAD = 32
 V_UNITS = ((0, 0), (0, 1), (1, 0), (1, 1))
 G_INTERLEAVES = (0, 1)
 N_G = 2
-S_W = (2,)
+W_BY = {0: "gg", 1: "gg", 2: "gs", 3: "sv", 4: "vv", 5: "vv", 6: "vv", 7: "vv"}
 
 
 def tile_routed_moe_kernel(tc, xT, w, b, gate, offs, pos1, pos2, out):
@@ -95,7 +95,9 @@ def tile_routed_moe_kernel(tc, xT, w, b, gate, offs, pos1, pos2, out):
         load_planes(1, (2,))
         load_pass_plane(3, 3)
         load_planes(1, (3,))
-        for e in range(2, E):
+        load_w_half(2, 0)
+        load_w_half(2, 1)
+        for e in range(3, E):
             load_w(e)
         nc.sync.dma_start(pos1_t[:], pos1)
         nc.sync.dma_start(pos2_t[:], pos2)
@@ -166,28 +168,34 @@ def tile_routed_moe_kernel(tc, xT, w, b, gate, offs, pos1, pos2, out):
         def quantize_scalar_pass(g, e0, e1):
             quantize_x(g, e0, e1, qs[g][:].rearrange("p j t -> p (j t)")[:, e0 * 4 * C : e1 * 4 * C])
 
-        def interleave_w(e):
-            if e < N_G:
-                wq = wq_g[:, e, :, :]
-            elif e in S_W:
-                wq = keep.tile([P, G, 4 * N], BF16, name="wq%d" % e, align_bytes=64)[:]
-            else:
-                wq = keep.tile([P, G, 4 * N], BF16, name="wq%d" % e, tag=("win10", "win11", "wq_third")[e % 3], align_bytes=64)[:]
-            w_grouped[e] = wq
-            dst = wq.rearrange("p g (n t) -> p g n t", t=4)
-            src = wr[e][:].rearrange("p g (t n) -> p g n t", t=4)
-            if e < N_G:
-                for u in range(2):
+        def wq_of(e):
+            if e not in w_grouped:
+                if e < N_G:
+                    w_grouped[e] = wq_g[:, e, :, :]
+                elif "v" not in W_BY[e]:
+                    w_grouped[e] = keep.tile([P, G, 4 * N], BF16, name="wq%d" % e, align_bytes=64)[:]
+                else:
+                    w_grouped[e] = keep.tile(
+                        [P, G, 4 * N], BF16, name="wq%d" % e, tag=("win10", "win11", "wq_third")[e % 3], align_bytes=64
+                    )[:]
+            return w_grouped[e]
+
+        def interleave_w(e, engine):
+            wq = wq_of(e)
+            halves = [u for u in range(2) if W_BY[e][u] == engine]
+            if engine == "g":
+                dst = wq.rearrange("p g (n t) -> p g n t", t=4)
+                src = wr[e][:].rearrange("p g (t n) -> p g n t", t=4)
+                for u in halves:
                     nc.gpsimd.tensor_scalar(dst[:, 2 * u : 2 * u + 2], src[:, 2 * u : 2 * u + 2], 1.0, 0.0, MULT, ADD)
-            elif e in S_W:
-                nc.scalar.copy(
-                    out=wq.rearrange("p g (c i t) -> p g c t i", i=4, t=4),
-                    in_=wr[e][:].rearrange("p g (t c i) -> p g c t i", t=4, i=4),
-                )
             else:
-                dst = wq.rearrange("p g (c i t) -> p g c t i", i=4, t=4)
-                src = wr[e][:].rearrange("p g (t c i) -> p g c t i", t=4, i=4)
-                nc.vector.tensor_copy(out=dst, in_=src)
+                lo, hi = 2 * halves[0], 2 * halves[-1] + 2
+                dst = wq[:, lo:hi, :].rearrange("p g (c i t) -> p g c t i", i=4, t=4)
+                src = wr[e][:, lo:hi, :].rearrange("p g (t c i) -> p g c t i", t=4, i=4)
+                if engine == "s":
+                    nc.scalar.copy(out=dst, in_=src)
+                else:
+                    nc.vector.tensor_copy(out=dst, in_=src)
 
         def quantize_w(e):
             nc.vector.quantize_mx(
@@ -220,11 +228,12 @@ def tile_routed_moe_kernel(tc, xT, w, b, gate, offs, pos1, pos2, out):
         xs = scales[:, 0 : G * S].rearrange("p (g s) -> p g s", g=G)
         ws = scales[:, G * S : 2 * G * S].rearrange("p (e c) -> p e c", e=E)
         nc.gpsimd.tensor_scalar(xb[3][:, 1, :], xraw[3][:, 1, :], 1.0, 0.0, MULT, ADD)
-        interleave_w(0)
-        interleave_w(1)
+        interleave_w(0, "g")
+        interleave_w(1, "g")
         interleave(0)
         nc.gpsimd.tensor_scalar(xb[2][:], xraw[2][:], 1.0, 0.0, MULT, ADD)
         interleave(1)
+        interleave_w(2, "g")
 
         for t in range(4):
             if t != 1:
@@ -235,14 +244,16 @@ def tile_routed_moe_kernel(tc, xT, w, b, gate, offs, pos1, pos2, out):
             interleave(i)
 
         quantize_w_gpsimd()
-        interleave_w(N_G)
+        interleave_w(2, "s")
         quantize_x(0, 0, E, qt_g[:])
         quantize_x(1, 0, 4, qt[2])
         quantize_x(1, 4, E, qt[3])
         quantize_scalar_pass(3, 0, E)
         for e in range(N_G, E):
             if e + 1 < E:
-                interleave_w(e + 1)
+                for engine in ("s", "v"):
+                    if engine in W_BY[e + 1]:
+                        interleave_w(e + 1, engine)
             quantize_w(e)
 
         for e in range(E):

@@ -249,6 +249,9 @@ def tile_routed_moe_kernel(tc, xT, w, b, gate, offs, pos1, pos2, out):
         quantize_x(1, 0, 4, qt[2])
         quantize_x(1, 4, E, qt[3])
         quantize_scalar_pass(3, 0, E)
+        for e in range(2):
+            for t in range(4):
+                scalar_gather(2, t, e)
         for e in range(N_G, E):
             if e + 1 < E:
                 for engine in ("s", "v"):
@@ -256,7 +259,7 @@ def tile_routed_moe_kernel(tc, xT, w, b, gate, offs, pos1, pos2, out):
                         interleave_w(e + 1, engine)
             quantize_w(e)
 
-        for e in range(E):
+        for e in range(2, E):
             for t in range(4):
                 scalar_gather(2, t, e)
         y = keep.tile([P, S], F32, name="y", tag="xb2")

@@ -123,8 +123,8 @@ def tile_routed_moe_kernel(tc, xT, w, b, gate, offs, pos1, pos2, out):
 
         def interleave(i):
             if i in G_INTERLEAVES:
-                dst = qt[i].rearrange("p (j t) -> p j t", t=4)
-                src = gathered[i][:].rearrange("p t j -> p j t")
+                dst = qt[i].rearrange("p (c i t) -> p c t i", i=4, t=4)
+                src = gathered[i][:].rearrange("p t (c i) -> p c t i", i=4)
                 nc.gpsimd.tensor_scalar(dst, src, 1.0, 0.0, MULT, ADD)
             else:
                 dst = qt[i].rearrange("p (c i t) -> p c t i", i=4, t=4)

@@ -25,7 +25,7 @@ PAD = 32
 V_UNITS = ((0, 0), (0, 1), (1, 0), (1, 1))
 G_INTERLEAVES = (0, 1)
 N_G = 2
-W_BY = {0: "gg", 1: "gg", 2: "gs", 3: "sv", 4: "vv", 5: "vv", 6: "vv", 7: "vv"}
+W_BY = {0: "gggg", 1: "gggg", 2: "gsss", 3: "svvv", 4: "vvvv", 5: "vvvv", 6: "vvvv", 7: "vvvv"}
 
 
 def tile_routed_moe_kernel(tc, xT, w, b, gate, offs, pos1, pos2, out):
@@ -95,8 +95,8 @@ def tile_routed_moe_kernel(tc, xT, w, b, gate, offs, pos1, pos2, out):
         load_planes(1, (2,))
         load_pass_plane(3, 3)
         load_planes(1, (3,))
-        load_w_half(2, 0)
-        load_w_half(2, 1)
+        nc.sync.dma_start(out=wr[2][:, 0:1, :], in_=wv[2][:, 0:1, :])
+        nc.sync.dma_start(out=wr[2][:, 1:G, :], in_=wv[2][:, 1:G, :])
         for e in range(3, E):
             load_w(e)
         nc.sync.dma_start(pos1_t[:], pos1)
@@ -182,17 +182,25 @@ def tile_routed_moe_kernel(tc, xT, w, b, gate, offs, pos1, pos2, out):
 
         def interleave_w(e, engine):
             wq = wq_of(e)
-            halves = [u for u in range(2) if W_BY[e][u] == engine]
-            if engine == "g":
+            passes = [g for g in range(G) if W_BY[e][g] == engine]
+            lo, hi = passes[0], passes[-1] + 1
+            if engine == "g" and hi - lo > 1:
                 dst = wq.rearrange("p g (n t) -> p g n t", t=4)
                 src = wr[e][:].rearrange("p g (t n) -> p g n t", t=4)
-                for u in halves:
-                    nc.gpsimd.tensor_scalar(dst[:, 2 * u : 2 * u + 2], src[:, 2 * u : 2 * u + 2], 1.0, 0.0, MULT, ADD)
-            else:
-                lo, hi = 2 * halves[0], 2 * halves[-1] + 2
-                dst = wq[:, lo:hi, :].rearrange("p g (c i t) -> p g c t i", i=4, t=4)
-                src = wr[e][:, lo:hi, :].rearrange("p g (t c i) -> p g c t i", t=4, i=4)
-                if engine == "s":
+                for u in range(lo, hi, 2):
+                    nc.gpsimd.tensor_scalar(dst[:, u : u + 2], src[:, u : u + 2], 1.0, 0.0, MULT, ADD)
+                return
+            pieces = [(lo, lo + 1), (lo + 1, hi)] if engine == "v" and (hi - lo) % 2 == 1 and hi - lo > 1 else [(lo, hi)]
+            for (g0, g1) in pieces:
+                if g1 - g0 == 1:
+                    dst = wq[:, g0, :].rearrange("p (c i t) -> p c t i", i=4, t=4)
+                    src = wr[e][:, g0, :].rearrange("p (t c i) -> p c t i", t=4, i=4)
+                else:
+                    dst = wq[:, g0:g1, :].rearrange("p g (c i t) -> p g c t i", i=4, t=4)
+                    src = wr[e][:, g0:g1, :].rearrange("p g (t c i) -> p g c t i", t=4, i=4)
+                if engine == "g":
+                    nc.gpsimd.tensor_scalar(dst, src, 1.0, 0.0, MULT, ADD)
+                elif engine == "s":
                     nc.scalar.copy(out=dst, in_=src)
                 else:
                     nc.vector.tensor_copy(out=dst, in_=src)

@@ -260,19 +260,24 @@ def tile_routed_moe_kernel(tc, xT, w, b, gate, offs, pos1, pos2, out):
         for e in range(2):
             for t in range(4):
                 scalar_gather(2, t, e)
-        for e in range(N_G, E):
-            if e + 1 < E:
-                for engine in ("s", "v"):
-                    if engine in W_BY[e + 1]:
-                        interleave_w(e + 1, engine)
+        for e in range(N_G, E - 3):
+            for engine in ("s", "v"):
+                if engine in W_BY[e + 1]:
+                    interleave_w(e + 1, engine)
             quantize_w(e)
 
         for e in range(2, E):
             for t in range(4):
                 scalar_gather(2, t, e)
         y = keep.tile([P, S], F32, name="y", tag="xb2")
-        for e0 in range(0, E - 2, 2):
-            quantize_scalar_pass(2, e0, e0 + 2)
+        interleave_w(E - 2, "v")
+        quantize_w(E - 3)
+        quantize_scalar_pass(2, 0, 2)
+        interleave_w(E - 1, "v")
+        quantize_w(E - 2)
+        quantize_scalar_pass(2, 2, 4)
+        quantize_w(E - 1)
+        quantize_scalar_pass(2, 4, 6)
         quantize_scalar_pass(2, E - 2, E - 1)
         quantize_scalar_pass(2, E - 1, E)
 

@@ -121,6 +121,11 @@ def tile_routed_moe_kernel(tc, xT, w, b, gate, offs, pos1, pos2, out):
             col = h * HALF // 16
             nc.vector.tensor_copy(gathered[i][:, t, :], xp[g][t][:].indirect(offs_t[:, col : col + HALF // 16]))
 
+        def interleave_pass0():
+            dst = qt_g[:].rearrange("p (c i t) -> p c t i", i=4, t=4)
+            src = gt01[:].rearrange("p t (c i) -> p c t i", i=4)
+            nc.gpsimd.tensor_scalar(dst, src, 1.0, 0.0, MULT, ADD)
+
         def interleave(i):
             if i in G_INTERLEAVES:
                 dst = qt[i].rearrange("p (c i t) -> p c t i", i=4, t=4)
@@ -221,8 +226,11 @@ def tile_routed_moe_kernel(tc, xT, w, b, gate, offs, pos1, pos2, out):
             done_w.extend(range(N_G))
             matmuls()
 
-        for i in range(len(V_UNITS)):
-            gathered[i] = ring.tile([P, 4, HALF], F32, name="gt%d" % i, tag="gt", bufs=4)
+        gt01 = keep.tile([P, 4, 2 * HALF], F32, name="gt01", tag="gt01")
+        gathered[0] = gt01[:, :, 0:HALF]
+        gathered[1] = gt01[:, :, HALF : 2 * HALF]
+        for i in (2, 3):
+            gathered[i] = ring.tile([P, 4, HALF], F32, name="gt%d" % i, tag="gt", bufs=2)
         for g in range(2):
             for t in range(4):
                 for h in range(2):
@@ -238,9 +246,8 @@ def tile_routed_moe_kernel(tc, xT, w, b, gate, offs, pos1, pos2, out):
         nc.gpsimd.tensor_scalar(xb[3][:, 1, :], xraw[3][:, 1, :], 1.0, 0.0, MULT, ADD)
         interleave_w(0, "g")
         interleave_w(1, "g")
-        interleave(0)
+        interleave_pass0()
         nc.gpsimd.tensor_scalar(xb[2][:], xraw[2][:], 1.0, 0.0, MULT, ADD)
-        interleave(1)
         interleave_w(2, "g")
 
         for t in range(4):
@@ -281,9 +288,9 @@ def tile_routed_moe_kernel(tc, xT, w, b, gate, offs, pos1, pos2, out):
         quantize_scalar_pass(2, E - 2, E - 1)
         quantize_scalar_pass(2, E - 1, E)
 
-        t1 = ring.tile([P, T], F32, name="t1", tag="gt", bufs=4)
-        t2 = ring.tile([P, T], F32, name="t2", tag="gt", bufs=4)
-        res = ring.tile([P, T], F32, name="res", tag="gt", bufs=4)
+        t1 = keep.tile([P, T], F32, name="t1", tag="gt01")
+        t2 = ring.tile([P, T], F32, name="t2", tag="gt", bufs=2)
+        res = ring.tile([P, T], F32, name="res", tag="gt", bufs=2)
         nc.vector.tensor_tensor(t1[:], y[:].indirect(pos1_t[:]), gate0[:], MULT)
         for c0 in (0, T // 2):
             cols = slice(c0, c0 + T // 2)

@@ -25,6 +25,8 @@ PAD = 32
 V_UNITS = ((0, 0), (0, 1), (1, 0), (1, 1))
 G_INTERLEAVES = (0, 1)
 N_G = 2
+PASS2_TILES = ((0, 2), (2, 4), (4, 5), (5, 6), (6, 7), (7, 8))
+W_TAG = {3: "win10", 4: "qs2_0", 5: "win11", 6: "qs2_2"}
 W_BY = {0: "gggg", 1: "gggg", 2: "gsss", 3: "svvv", 4: "vvvv", 5: "vvvv", 6: "vvvv", 7: "vvvv"}
 
 
@@ -46,7 +48,11 @@ def tile_routed_moe_kernel(tc, xT, w, b, gate, offs, pos1, pos2, out):
         ]
         xraw = {g: keep.tile([P, 4, T], F32, name="xraw%d" % g) for g in (2, 3)}
         xb = {g: keep.tile([P, 4, T], BF16, name="xb%d" % g, tag="xb%d" % g) for g in (2, 3)}
-        qs = {g: keep.tile([P, S, 4], BF16, name="qs%d" % g, align_bytes=64) for g in (2, 3)}
+        qs = {3: keep.tile([P, S, 4], BF16, name="qs3", align_bytes=64)}
+        qs2 = {
+            r: keep.tile([P, (r[1] - r[0]) * C, 4], BF16, name="qs2_%d" % r[0], tag="qs2_%d" % r[0], align_bytes=64)
+            for r in PASS2_TILES
+        }
         wr = [keep.tile([P, G, 4 * N], F32, name="wr%d" % e) for e in range(E)]
         xc = keep.tile([P, G, S], U32, name="xc", align_bytes=64)
         wc = keep.tile([P, E, G * N], U32, name="wc", align_bytes=64)
@@ -137,16 +143,21 @@ def tile_routed_moe_kernel(tc, xT, w, b, gate, offs, pos1, pos2, out):
                 nc.vector.tensor_copy(out=dst, in_=src)
 
         def scalar_gather(g, t, e):
+            if g == 2:
+                r = [q for q in PASS2_TILES if q[0] <= e < q[1]][0]
+                dst = qs2[r][:, (e - r[0]) * C : (e - r[0] + 1) * C, t]
+            else:
+                dst = qs[g][:, e * C : (e + 1) * C, t]
             nc.scalar.activation(
-                qs[g][:, e * C : (e + 1) * C, t],
+                dst,
                 xb[g][:, t, :].indirect(offs_t[:, e * C // 16 : (e + 1) * C // 16]),
                 COPY,
             )
 
         def matmuls():
             for (g, e0, e1) in done_x:
-                for e in done_w:
-                    if e < e0 or e >= e1 or (e, g) in issued:
+                for (e, g0, g1) in done_w:
+                    if e < e0 or e >= e1 or g < g0 or g >= g1 or (e, g) in issued:
                         continue
                     count = len([1 for key in issued if key[0] == e])
                     issued[(e, g)] = True
@@ -171,7 +182,10 @@ def tile_routed_moe_kernel(tc, xT, w, b, gate, offs, pos1, pos2, out):
             matmuls()
 
         def quantize_scalar_pass(g, e0, e1):
-            quantize_x(g, e0, e1, qs[g][:].rearrange("p j t -> p (j t)")[:, e0 * 4 * C : e1 * 4 * C])
+            if g == 2:
+                quantize_x(g, e0, e1, qs2[(e0, e1)][:].rearrange("p j t -> p (j t)"))
+            else:
+                quantize_x(g, e0, e1, qs[g][:].rearrange("p j t -> p (j t)")[:, e0 * 4 * C : e1 * 4 * C])
 
         def wq_of(e):
             if e not in w_grouped:
@@ -181,7 +195,7 @@ def tile_routed_moe_kernel(tc, xT, w, b, gate, offs, pos1, pos2, out):
                     w_grouped[e] = keep.tile([P, G, 4 * N], BF16, name="wq%d" % e, align_bytes=64)[:]
                 else:
                     w_grouped[e] = keep.tile(
-                        [P, G, 4 * N], BF16, name="wq%d" % e, tag=("win10", "win11", "wq_third")[e % 3], align_bytes=64
+                        [P, G, 4 * N], BF16, name="wq%d" % e, tag=W_TAG[e], align_bytes=64
                     )[:]
             return w_grouped[e]
 
@@ -214,7 +228,23 @@ def tile_routed_moe_kernel(tc, xT, w, b, gate, offs, pos1, pos2, out):
             nc.vector.quantize_mx(
                 out=wc[:, e, :].bitcast(FP8X4), scales=ws[:, e, :], in_=w_grouped[e].rearrange("p g c -> p (g c)")
             )
-            done_w.append(e)
+            done_w.append((e, 0, G))
+            matmuls()
+
+        w7 = {}
+
+        def interleave_w7(u):
+            w7[u] = keep.tile([P, 2, 4 * N], BF16, name="wq7_%d" % u, tag="qs2_%d" % (4 + u), align_bytes=64)
+            dst = w7[u][:].rearrange("p g (c i t) -> p g c t i", i=4, t=4)
+            src = wr[E - 1][:, 2 * u : 2 * u + 2, :].rearrange("p g (t c i) -> p g c t i", t=4, i=4)
+            nc.vector.tensor_copy(out=dst, in_=src)
+
+        def quantize_w7(u):
+            cols = slice(2 * u * N, (2 * u + 2) * N)
+            nc.vector.quantize_mx(
+                out=wc[:, E - 1, cols].bitcast(FP8X4), scales=ws[:, E - 1, cols], in_=w7[u][:].rearrange("p g c -> p (g c)")
+            )
+            done_w.append((E - 1, 2 * u, 2 * u + 2))
             matmuls()
 
         def quantize_w_gpsimd():
@@ -223,7 +253,7 @@ def tile_routed_moe_kernel(tc, xT, w, b, gate, offs, pos1, pos2, out):
                 scales=ws[:, 0:N_G, :].rearrange("p e c -> p (e c)"),
                 in_=wq_g[:].rearrange("p e g c -> p (e g c)"),
             )
-            done_w.extend(range(N_G))
+            done_w.extend([(e, 0, G) for e in range(N_G)])
             matmuls()
 
         gt01 = keep.tile([P, 4, 2 * HALF], F32, name="gt01", tag="gt01")
@@ -267,26 +297,30 @@ def tile_routed_moe_kernel(tc, xT, w, b, gate, offs, pos1, pos2, out):
         for e in range(2):
             for t in range(4):
                 scalar_gather(2, t, e)
-        for e in range(N_G, E - 3):
-            for engine in ("s", "v"):
-                if engine in W_BY[e + 1]:
-                    interleave_w(e + 1, engine)
-            quantize_w(e)
-
+        interleave_w(3, "s")
         for e in range(2, E):
             for t in range(4):
                 scalar_gather(2, t, e)
         y = keep.tile([P, S], F32, name="y", tag="xb2")
-        interleave_w(E - 2, "v")
-        quantize_w(E - 3)
+        interleave_w(3, "v")
         quantize_scalar_pass(2, 0, 2)
-        interleave_w(E - 1, "v")
-        quantize_w(E - 2)
+        quantize_w(2)
+        interleave_w(4, "v")
+        quantize_w(3)
+        interleave_w(5, "v")
         quantize_scalar_pass(2, 2, 4)
-        quantize_w(E - 1)
-        quantize_scalar_pass(2, 4, 6)
-        quantize_scalar_pass(2, E - 2, E - 1)
-        quantize_scalar_pass(2, E - 1, E)
+        quantize_w(4)
+        interleave_w(6, "v")
+        quantize_scalar_pass(2, 4, 5)
+        quantize_w(5)
+        interleave_w7(0)
+        quantize_scalar_pass(2, 5, 6)
+        quantize_w(6)
+        interleave_w7(1)
+        quantize_w7(0)
+        quantize_scalar_pass(2, 6, 7)
+        quantize_w7(1)
+        quantize_scalar_pass(2, 7, 8)
 
         t1 = keep.tile([P, T], F32, name="t1", tag="gt01")
         t2 = ring.tile([P, T], F32, name="t2", tag="gt", bufs=2)

@@ -20,6 +20,7 @@ P = 128
 G = 4
 S = E * C
 HALF = 512
+FIRST = 384
 PAD = 32
 
 V_UNITS = ((0, 0), (0, 1), (1, 0), (1, 1))
@@ -83,8 +84,8 @@ def tile_routed_moe_kernel(tc, xT, w, b, gate, offs, pos1, pos2, out):
         def load_w_half(e, u):
             nc.sync.dma_start(out=wr[e][:, 2 * u : 2 * u + 2, :], in_=wv[e][:, 2 * u : 2 * u + 2, :])
 
-        nc.sync.dma_start(offs_t[:], offs)
         load_planes(0, (0,))
+        nc.sync.dma_start(offs_t[:], offs)
         load_pass_plane(3, 0)
         load_planes(0, (1,))
         load_pass_plane(3, 1)
@@ -273,6 +274,7 @@ def tile_routed_moe_kernel(tc, xT, w, b, gate, offs, pos1, pos2, out):
         wq_g = keep.tile([P, N_G, G, 4 * N], BF16, name="wq_g", align_bytes=64)
         xs = scales[:, 0 : G * S].rearrange("p (g s) -> p g s", g=G)
         ws = scales[:, G * S : 2 * G * S].rearrange("p (e c) -> p e c", e=E)
+        nc.gpsimd.tensor_scalar(xb[3][:, 0, FIRST:T], xraw[3][:, 0, FIRST:T], 1.0, 0.0, MULT, ADD)
         nc.gpsimd.tensor_scalar(xb[3][:, 1, :], xraw[3][:, 1, :], 1.0, 0.0, MULT, ADD)
         interleave_w(0, "g")
         interleave_w(1, "g")
@@ -281,7 +283,9 @@ def tile_routed_moe_kernel(tc, xT, w, b, gate, offs, pos1, pos2, out):
         interleave_w(2, "g")
 
         for t in range(4):
-            if t != 1:
+            if t == 0:
+                nc.scalar.copy(out=xb[3][:, t, 0:FIRST], in_=xraw[3][:, t, 0:FIRST])
+            elif t != 1:
                 nc.scalar.copy(out=xb[3][:, t, :], in_=xraw[3][:, t, :])
             for e in range(E):
                 scalar_gather(3, t, e)

@@ -28,6 +28,7 @@ G_INTERLEAVES = (0, 1)
 N_G = 2
 PASS2_TILES = ((0, 2), (2, 4), (4, 5), (5, 6), (6, 7), (7, 8))
 W_TAG = {3: "win10", 4: "qs2_0", 5: "win11", 6: "qs2_2"}
+SHARED = (3, 1, 16)
 W_BY = {0: "gggg", 1: "gggg", 2: "gsss", 3: "svvv", 4: "vvvv", 5: "vvvv", 6: "vvvv", 7: "vvvv"}
 
 
@@ -215,6 +216,9 @@ def tile_routed_moe_kernel(tc, xT, w, b, gate, offs, pos1, pos2, out):
                 if g1 - g0 == 1:
                     dst = wq[:, g0, :].rearrange("p (c i t) -> p c t i", i=4, t=4)
                     src = wr[e][:, g0, :].rearrange("p (t c i) -> p c t i", t=4, i=4)
+                    if engine == "v" and (e, g0) == SHARED[0:2]:
+                        dst = dst[:, SHARED[2] :]
+                        src = src[:, SHARED[2] :]
                 else:
                     dst = wq[:, g0:g1, :].rearrange("p g (c i t) -> p g c t i", i=4, t=4)
                     src = wr[e][:, g0:g1, :].rearrange("p g (t c i) -> p g c t i", t=4, i=4)
@@ -302,6 +306,10 @@ def tile_routed_moe_kernel(tc, xT, w, b, gate, offs, pos1, pos2, out):
             for t in range(4):
                 scalar_gather(2, t, e)
         interleave_w(3, "s")
+        nc.scalar.copy(
+            out=wq_of(SHARED[0])[:, SHARED[1], :].rearrange("p (c i t) -> p c t i", i=4, t=4)[:, 0 : SHARED[2]],
+            in_=wr[SHARED[0]][:, SHARED[1], :].rearrange("p (t c i) -> p c t i", t=4, i=4)[:, 0 : SHARED[2]],
+        )
         for e in range(2, E):
             for t in range(4):
                 scalar_gather(2, t, e)

@@ -45,19 +45,19 @@ def tile_routed_moe_kernel(tc, xT, w, b, gate, offs, pos1, pos2, out):
         pos2_t = lists.tile([P, T // 16], U16, name="pos2_t")
 
         xp = [
-            [keep.tile([P, T + PAD], F32, name="xp%d%d" % (g, t), tag="win%d%d" % (g, t), align_bytes=64) for t in range(4)]
+            [keep.tile([P, T + PAD], F32, name="xp%d%d" % (g, t), tag="win%d%d" % (g, t), align_bytes=256) for t in range(4)]
             for g in range(2)
         ]
         xraw = {g: keep.tile([P, 4, T], F32, name="xraw%d" % g) for g in (2, 3)}
         xb = {g: keep.tile([P, 4, T], BF16, name="xb%d" % g, tag="xb%d" % g) for g in (2, 3)}
-        qs = {3: keep.tile([P, S, 4], BF16, name="qs3", align_bytes=64)}
+        qs = {3: keep.tile([P, S, 4], BF16, name="qs3", align_bytes=256)}
         qs2 = {
-            r: keep.tile([P, (r[1] - r[0]) * C, 4], BF16, name="qs2_%d" % r[0], tag="qs2_%d" % r[0], align_bytes=64)
+            r: keep.tile([P, (r[1] - r[0]) * C, 4], BF16, name="qs2_%d" % r[0], tag="qs2_%d" % r[0], align_bytes=256)
             for r in PASS2_TILES
         }
         wr = [keep.tile([P, G, 4 * N], F32, name="wr%d" % e) for e in range(E)]
-        xc = keep.tile([P, G, S], U32, name="xc", align_bytes=64)
-        wc = keep.tile([P, E, G * N], U32, name="wc", align_bytes=64)
+        xc = keep.tile([P, G, S], U32, name="xc", align_bytes=256)
+        wc = keep.tile([P, E, G * N], U32, name="wc", align_bytes=256)
         b_t = keep.tile([P, E], F32, name="b_t")
         gate0 = keep.tile([P, T], F32, name="gate0")
         gate1 = keep.tile([P, T], F32, name="gate1")
@@ -194,10 +194,10 @@ def tile_routed_moe_kernel(tc, xT, w, b, gate, offs, pos1, pos2, out):
                 if e < N_G:
                     w_grouped[e] = wq_g[:, e, :, :]
                 elif "v" not in W_BY[e]:
-                    w_grouped[e] = keep.tile([P, G, 4 * N], BF16, name="wq%d" % e, align_bytes=64)[:]
+                    w_grouped[e] = keep.tile([P, G, 4 * N], BF16, name="wq%d" % e, align_bytes=256)[:]
                 else:
                     w_grouped[e] = keep.tile(
-                        [P, G, 4 * N], BF16, name="wq%d" % e, tag=W_TAG[e], align_bytes=64
+                        [P, G, 4 * N], BF16, name="wq%d" % e, tag=W_TAG[e], align_bytes=256
                     )[:]
             return w_grouped[e]
 
@@ -239,7 +239,7 @@ def tile_routed_moe_kernel(tc, xT, w, b, gate, offs, pos1, pos2, out):
         w7 = {}
 
         def interleave_w7(u):
-            w7[u] = keep.tile([P, 2, 4 * N], BF16, name="wq7_%d" % u, tag="qs2_%d" % (4 + u), align_bytes=64)
+            w7[u] = keep.tile([P, 2, 4 * N], BF16, name="wq7_%d" % u, tag="qs2_%d" % (4 + u), align_bytes=256)
             dst = w7[u][:].rearrange("p g (c i t) -> p g c t i", i=4, t=4)
             src = wr[E - 1][:, 2 * u : 2 * u + 2, :].rearrange("p g (t c i) -> p g c t i", t=4, i=4)
             nc.vector.tensor_copy(out=dst, in_=src)
@@ -270,12 +270,12 @@ def tile_routed_moe_kernel(tc, xT, w, b, gate, offs, pos1, pos2, out):
             for t in range(4):
                 for h in range(2):
                     gather(2 * g + h, t)
-        scales = keep.tile([P, 2 * G * S], U8, name="scales", tag="win13", align_bytes=64)
-        qt_g = keep.tile([P, 2 * 4 * HALF], BF16, name="qt_g", align_bytes=64)
-        qt2 = keep.tile([P, 4 * HALF], BF16, name="qt2", tag="win12", align_bytes=64)
-        qt3 = keep.tile([P, 4 * HALF], BF16, name="qt3", align_bytes=64)
+        scales = keep.tile([P, 2 * G * S], U8, name="scales", tag="win13", align_bytes=256)
+        qt_g = keep.tile([P, 2 * 4 * HALF], BF16, name="qt_g", align_bytes=256)
+        qt2 = keep.tile([P, 4 * HALF], BF16, name="qt2", tag="win12", align_bytes=256)
+        qt3 = keep.tile([P, 4 * HALF], BF16, name="qt3", align_bytes=256)
         qt = [qt_g[:, 0 : 4 * HALF], qt_g[:, 4 * HALF : 2 * 4 * HALF], qt2[:], qt3[:]]
-        wq_g = keep.tile([P, N_G, G, 4 * N], BF16, name="wq_g", align_bytes=64)
+        wq_g = keep.tile([P, N_G, G, 4 * N], BF16, name="wq_g", align_bytes=256)
         xs = scales[:, 0 : G * S].rearrange("p (g s) -> p g s", g=G)
         ws = scales[:, G * S : 2 * G * S].rearrange("p (e c) -> p e c", e=E)
         nc.gpsimd.tensor_scalar(xb[3][:, 0, FIRST:T], xraw[3][:, 0, FIRST:T], 1.0, 0.0, MULT, ADD)

@@ -239,7 +239,7 @@ def tile_routed_moe_kernel(tc, xT, w, b, gate, offs, pos1, pos2, out):
         w7 = {}
 
         def interleave_w7(u):
-            w7[u] = keep.tile([P, 2, 4 * N], BF16, name="wq7_%d" % u, tag="qs2_%d" % (4 + u), align_bytes=256)
+            w7[u] = keep.tile([P, 2, 4 * N], BF16, name="wq7_%d" % u, tag=("win11", "qs2_2")[u], align_bytes=256)
             dst = w7[u][:].rearrange("p g (c i t) -> p g c t i", i=4, t=4)
             src = wr[E - 1][:, 2 * u : 2 * u + 2, :].rearrange("p g (t c i) -> p g c t i", t=4, i=4)
             nc.vector.tensor_copy(out=dst, in_=src)
@@ -323,13 +323,13 @@ def tile_routed_moe_kernel(tc, xT, w, b, gate, offs, pos1, pos2, out):
         quantize_scalar_pass(2, 2, 4)
         quantize_w(4)
         interleave_w(6, "v")
-        quantize_scalar_pass(2, 4, 5)
         quantize_w(5)
-        interleave_w7(0)
-        quantize_scalar_pass(2, 5, 6)
         quantize_w(6)
-        interleave_w7(1)
+        interleave_w7(0)
+        quantize_scalar_pass(2, 4, 5)
+        quantize_scalar_pass(2, 5, 6)
         quantize_w7(0)
+        interleave_w7(1)
         quantize_scalar_pass(2, 6, 7)
         quantize_w7(1)
         quantize_scalar_pass(2, 7, 8)

@@ -302,15 +302,18 @@ def tile_routed_moe_kernel(tc, xT, w, b, gate, offs, pos1, pos2, out):
         quantize_x(1, 0, 4, qt[2])
         quantize_x(1, 4, E, qt[3])
         quantize_scalar_pass(3, 0, E)
-        for e in range(2):
-            for t in range(4):
+        for t in range(4):
+            for e in range(2):
                 scalar_gather(2, t, e)
         interleave_w(3, "s")
         nc.scalar.copy(
             out=wq_of(SHARED[0])[:, SHARED[1], :].rearrange("p (c i t) -> p c t i", i=4, t=4)[:, 0 : SHARED[2]],
             in_=wr[SHARED[0]][:, SHARED[1], :].rearrange("p (t c i) -> p c t i", t=4, i=4)[:, 0 : SHARED[2]],
         )
-        for e in range(2, E):
+        for t in range(4):
+            for e in range(2, 4):
+                scalar_gather(2, t, e)
+        for e in range(4, E):
             for t in range(4):
                 scalar_gather(2, t, e)
         y = keep.tile([P, S], F32, name="y", tag="xb2")

@@ -93,8 +93,8 @@ def tile_routed_moe_kernel(tc, xT, w, b, gate, offs, pos1, pos2, out):
         load_w_half(0, 0)
         load_planes(0, (2,))
         load_w_half(0, 1)
-        load_planes(0, (3,))
         load_w_half(1, 0)
+        load_planes(0, (3,))
         load_w_half(1, 1)
         load_planes(1, (0,))
         load_pass_plane(3, 2)

from contextlib import ExitStack

import concourse.mybir as mybir

K, T, E, C, N = 2048, 512, 8, 128, 128
FLOPS = 2 * K * N * E * C

F32 = mybir.dt.float32
BF16 = mybir.dt.bfloat16
U32 = mybir.dt.uint32
U16 = mybir.dt.uint16
U8 = mybir.dt.uint8
FP8X4 = mybir.dt.float8_e4m3fn_x4
MULT = mybir.AluOpType.mult
ADD = mybir.AluOpType.add
GELU = mybir.ActivationFunctionType.Gelu_apprx_tanh
COPY = mybir.ActivationFunctionType.Copy

P = 128
G = 4
S = E * C
HALF = 512
FIRST = 384
PAD = 32

V_UNITS = ((0, 0), (0, 1), (1, 0), (1, 1))
G_INTERLEAVES = (0, 1)
N_G = 2
PASS2_TILES = ((0, 2), (2, 4), (4, 5), (5, 6), (6, 7), (7, 8))
W_TAG = {3: "win10", 4: "qs2_0", 5: "win11", 6: "qs2_2"}
SHARED = (3, 1, 16)
W_BY = {0: "gggg", 1: "gggg", 2: "gsss", 3: "svvv", 4: "vvvv", 5: "vvvv", 6: "vvvv", 7: "vvvv"}


def tile_routed_moe_kernel(tc, xT, w, b, gate, offs, pos1, pos2, out):
    nc = tc.nc
    with ExitStack() as ctx:
        lists = ctx.enter_context(tc.tile_pool(name="lists", bufs=1))
        keep = ctx.enter_context(tc.tile_pool(name="keep", bufs=1))
        ring = ctx.enter_context(tc.tile_pool(name="ring", bufs=3))
        psum = ctx.enter_context(tc.psum_pool(name="psum", bufs=1))

        offs_t = lists.tile([P, S // 16], U16, name="offs_t")
        pos1_t = lists.tile([P, T // 16], U16, name="pos1_t")
        pos2_t = lists.tile([P, T // 16], U16, name="pos2_t")

        xp = [
            [keep.tile([P, T + PAD], F32, name="xp%d%d" % (g, t), tag="win%d%d" % (g, t), align_bytes=256) for t in range(4)]
            for g in range(2)
        ]
        xraw = {g: keep.tile([P, 4, T], F32, name="xraw%d" % g) for g in (2, 3)}
        xb = {g: keep.tile([P, 4, T], BF16, name="xb%d" % g, tag="xb%d" % g) for g in (2, 3)}
        qs = {3: keep.tile([P, S, 4], BF16, name="qs3", align_bytes=256)}
        qs2 = {
            r: keep.tile([P, (r[1] - r[0]) * C, 4], BF16, name="qs2_%d" % r[0], tag="qs2_%d" % r[0], align_bytes=256)
            for r in PASS2_TILES
        }
        wr = [keep.tile([P, G, 4 * N], F32, name="wr%d" % e) for e in range(E)]
        xc = keep.tile([P, G, S], U32, name="xc", align_bytes=256)
        wc = keep.tile([P, E, G * N], U32, name="wc", align_bytes=256)
        b_t = keep.tile([P, E], F32, name="b_t")
        gate0 = keep.tile([P, T], F32, name="gate0")
        gate1 = keep.tile([P, T], F32, name="gate1")
        acc = [psum.tile([P, C], F32, name="acc%d" % e) for e in range(E)]

        xv = xT.rearrange("(g p t) n -> g p t n", p=P, t=4)
        xflat = xT.rearrange("k n -> (k n)")
        wv = w.rearrange("e (g p t) n -> e p g (t n)", p=P, t=4)

        def load_planes(g, planes):
            for t in planes:
                first = (512 * g + t) * T
                rows = xflat[first : first + P * 4 * T].rearrange("(p r) -> p r", r=4 * T)
                nc.sync.dma_start(out=xp[g][t][:], in_=rows[:, 0 : T + PAD])

        def load_pass(g):
            nc.sync.dma_start(out=xraw[g][:], in_=xv[g])

        def load_pass_plane(g, t):
            nc.sync.dma_start(out=xraw[g][:, t, :], in_=xv[g, :, t, :])

        def load_w(e):
            nc.sync.dma_start(out=wr[e][:], in_=wv[e])

        def load_w_half(e, u):
            nc.sync.dma_start(out=wr[e][:, 2 * u : 2 * u + 2, :], in_=wv[e][:, 2 * u : 2 * u + 2, :])

        load_planes(0, (0,))
        nc.sync.dma_start(offs_t[:], offs)
        load_pass_plane(3, 0)
        load_planes(0, (1,))
        load_pass_plane(3, 1)
        load_w_half(0, 0)
        load_planes(0, (2,))
        load_w_half(0, 1)
        load_w_half(1, 0)
        load_planes(0, (3,))
        load_w_half(1, 1)
        load_planes(1, (0,))
        load_pass_plane(3, 2)
        load_planes(1, (1,))
        load_pass(2)
        load_planes(1, (2,))
        load_pass_plane(3, 3)
        load_planes(1, (3,))
        nc.sync.dma_start(out=wr[2][:, 0:1, :], in_=wv[2][:, 0:1, :])
        nc.sync.dma_start(out=wr[2][:, 1:G, :], in_=wv[2][:, 1:G, :])
        for e in range(3, E):
            load_w(e)
        nc.sync.dma_start(pos1_t[:], pos1)
        nc.sync.dma_start(pos2_t[:], pos2)
        nc.sync.dma_start(out=b_t[:], in_=b)
        nc.sync.dma_start(out=gate0[:], in_=gate[0])
        nc.sync.dma_start(out=gate1[:], in_=gate[1])

        warm = keep.tile([P, 1], F32, name="warm")
        warm2 = keep.tile([P, 1], F32, name="warm2")
        nc.gpsimd.memset(warm[:], 0.0)
        nc.scalar.activation(out=warm2[:], in_=warm[:], func=GELU)

        gathered = {}
        w_grouped = {}
        done_x = []
        done_w = []
        issued = {}

        def gather(i, t):
            g, h = V_UNITS[i]
            col = h * HALF // 16
            nc.vector.tensor_copy(gathered[i][:, t, :], xp[g][t][:].indirect(offs_t[:, col : col + HALF // 16]))

        def interleave_pass0():
            dst = qt_g[:].rearrange("p (c i t) -> p c t i", i=4, t=4)
            src = gt01[:].rearrange("p t (c i) -> p c t i", i=4)
            nc.gpsimd.tensor_scalar(dst, src, 1.0, 0.0, MULT, ADD)

        def interleave(i):
            if i in G_INTERLEAVES:
                dst = qt[i].rearrange("p (c i t) -> p c t i", i=4, t=4)
                src = gathered[i][:].rearrange("p t (c i) -> p c t i", i=4)
                nc.gpsimd.tensor_scalar(dst, src, 1.0, 0.0, MULT, ADD)
            else:
                dst = qt[i].rearrange("p (c i t) -> p c t i", i=4, t=4)
                src = gathered[i][:].rearrange("p t (c i) -> p c t i", i=4)
                nc.vector.tensor_copy(out=dst, in_=src)

        def scalar_gather(g, t, e):
            if g == 2:
                r = [q for q in PASS2_TILES if q[0] <= e < q[1]][0]
                dst = qs2[r][:, (e - r[0]) * C : (e - r[0] + 1) * C, t]
            else:
                dst = qs[g][:, e * C : (e + 1) * C, t]
            nc.scalar.activation(
                dst,
                xb[g][:, t, :].indirect(offs_t[:, e * C // 16 : (e + 1) * C // 16]),
                COPY,
            )

        def matmuls():
            for (g, e0, e1) in done_x:
                for (e, g0, g1) in done_w:
                    if e < e0 or e >= e1 or g < g0 or g >= g1 or (e, g) in issued:
                        continue
                    count = len([1 for key in issued if key[0] == e])
                    issued[(e, g)] = True
                    nc.tensor.matmul_mx(
                        out=acc[e][:],
                        lhsT=wc[:, e, g * N : (g + 1) * N].bitcast(FP8X4),
                        lhsT_scale=ws[:, e, g * N : (g + 1) * N],
                        rhs=xc[:, g, e * C : (e + 1) * C].bitcast(FP8X4),
                        rhs_scale=xs[:, g, e * C : (e + 1) * C],
                        start=(count == 0),
                        stop=(count == G - 1),
                    )
                    if count == G - 1:
                        nc.scalar.activation(
                            out=y[:, e * C : (e + 1) * C], in_=acc[e][:], func=GELU, bias=b_t[:, e : e + 1]
                        )

        def quantize_x(g, e0, e1, src):
            cols = slice(e0 * C, e1 * C)
            nc.vector.quantize_mx(out=xc[:, g, cols].bitcast(FP8X4), scales=xs[:, g, cols], in_=src)
            done_x.append((g, e0, e1))
            matmuls()

        def quantize_scalar_pass(g, e0, e1):
            if g == 2:
                quantize_x(g, e0, e1, qs2[(e0, e1)][:].rearrange("p j t -> p (j t)"))
            else:
                quantize_x(g, e0, e1, qs[g][:].rearrange("p j t -> p (j t)")[:, e0 * 4 * C : e1 * 4 * C])

        def wq_of(e):
            if e not in w_grouped:
                if e < N_G:
                    w_grouped[e] = wq_g[:, e, :, :]
                elif "v" not in W_BY[e]:
                    w_grouped[e] = keep.tile([P, G, 4 * N], BF16, name="wq%d" % e, align_bytes=256)[:]
                else:
                    w_grouped[e] = keep.tile(
                        [P, G, 4 * N], BF16, name="wq%d" % e, tag=W_TAG[e], align_bytes=256
                    )[:]
            return w_grouped[e]

        def interleave_w(e, engine):
            wq = wq_of(e)
            passes = [g for g in range(G) if W_BY[e][g] == engine]
            lo, hi = passes[0], passes[-1] + 1
            if engine == "g" and hi - lo > 1:
                dst = wq.rearrange("p g (n t) -> p g n t", t=4)
                src = wr[e][:].rearrange("p g (t n) -> p g n t", t=4)
                for u in range(lo, hi, 2):
                    nc.gpsimd.tensor_scalar(dst[:, u : u + 2], src[:, u : u + 2], 1.0, 0.0, MULT, ADD)
                return
            pieces = [(lo, lo + 1), (lo + 1, hi)] if engine == "v" and (hi - lo) % 2 == 1 and hi - lo > 1 else [(lo, hi)]
            for (g0, g1) in pieces:
                if g1 - g0 == 1:
                    dst = wq[:, g0, :].rearrange("p (c i t) -> p c t i", i=4, t=4)
                    src = wr[e][:, g0, :].rearrange("p (t c i) -> p c t i", t=4, i=4)
                    if engine == "v" and (e, g0) == SHARED[0:2]:
                        dst = dst[:, SHARED[2] :]
                        src = src[:, SHARED[2] :]
                else:
                    dst = wq[:, g0:g1, :].rearrange("p g (c i t) -> p g c t i", i=4, t=4)
                    src = wr[e][:, g0:g1, :].rearrange("p g (t c i) -> p g c t i", t=4, i=4)
                if engine == "g":
                    nc.gpsimd.tensor_scalar(dst, src, 1.0, 0.0, MULT, ADD)
                elif engine == "s":
                    nc.scalar.copy(out=dst, in_=src)
                else:
                    nc.vector.tensor_copy(out=dst, in_=src)

        def quantize_w(e):
            nc.vector.quantize_mx(
                out=wc[:, e, :].bitcast(FP8X4), scales=ws[:, e, :], in_=w_grouped[e].rearrange("p g c -> p (g c)")
            )
            done_w.append((e, 0, G))
            matmuls()

        w7 = {}

        def interleave_w7(u):
            w7[u] = keep.tile([P, 2, 4 * N], BF16, name="wq7_%d" % u, tag=("win11", "qs2_2")[u], align_bytes=256)
            dst = w7[u][:].rearrange("p g (c i t) -> p g c t i", i=4, t=4)
            src = wr[E - 1][:, 2 * u : 2 * u + 2, :].rearrange("p g (t c i) -> p g c t i", t=4, i=4)
            nc.vector.tensor_copy(out=dst, in_=src)

        def quantize_w7(u):
            cols = slice(2 * u * N, (2 * u + 2) * N)
            nc.vector.quantize_mx(
                out=wc[:, E - 1, cols].bitcast(FP8X4), scales=ws[:, E - 1, cols], in_=w7[u][:].rearrange("p g c -> p (g c)")
            )
            done_w.append((E - 1, 2 * u, 2 * u + 2))
            matmuls()

        def quantize_w_gpsimd():
            nc.vector.quantize_mx(
                out=wc[:, 0:N_G, :].rearrange("p e c -> p (e c)").bitcast(FP8X4),
                scales=ws[:, 0:N_G, :].rearrange("p e c -> p (e c)"),
                in_=wq_g[:].rearrange("p e g c -> p (e g c)"),
            )
            done_w.extend([(e, 0, G) for e in range(N_G)])
            matmuls()

        gt01 = keep.tile([P, 4, 2 * HALF], F32, name="gt01", tag="gt01")
        gathered[0] = gt01[:, :, 0:HALF]
        gathered[1] = gt01[:, :, HALF : 2 * HALF]
        for i in (2, 3):
            gathered[i] = ring.tile([P, 4, HALF], F32, name="gt%d" % i, tag="gt", bufs=2)
        for g in range(2):
            for t in range(4):
                for h in range(2):
                    gather(2 * g + h, t)
        scales = keep.tile([P, 2 * G * S], U8, name="scales", tag="win13", align_bytes=256)
        qt_g = keep.tile([P, 2 * 4 * HALF], BF16, name="qt_g", align_bytes=256)
        qt2 = keep.tile([P, 4 * HALF], BF16, name="qt2", tag="win12", align_bytes=256)
        qt3 = keep.tile([P, 4 * HALF], BF16, name="qt3", align_bytes=256)
        qt = [qt_g[:, 0 : 4 * HALF], qt_g[:, 4 * HALF : 2 * 4 * HALF], qt2[:], qt3[:]]
        wq_g = keep.tile([P, N_G, G, 4 * N], BF16, name="wq_g", align_bytes=256)
        xs = scales[:, 0 : G * S].rearrange("p (g s) -> p g s", g=G)
        ws = scales[:, G * S : 2 * G * S].rearrange("p (e c) -> p e c", e=E)
        nc.gpsimd.tensor_scalar(xb[3][:, 0, FIRST:T], xraw[3][:, 0, FIRST:T], 1.0, 0.0, MULT, ADD)
        nc.gpsimd.tensor_scalar(xb[3][:, 1, :], xraw[3][:, 1, :], 1.0, 0.0, MULT, ADD)
        interleave_w(0, "g")
        interleave_w(1, "g")
        interleave_pass0()
        nc.gpsimd.tensor_scalar(xb[2][:], xraw[2][:], 1.0, 0.0, MULT, ADD)
        interleave_w(2, "g")

        for t in range(4):
            if t == 0:
                nc.scalar.copy(out=xb[3][:, t, 0:FIRST], in_=xraw[3][:, t, 0:FIRST])
            elif t != 1:
                nc.scalar.copy(out=xb[3][:, t, :], in_=xraw[3][:, t, :])
            for e in range(E):
                scalar_gather(3, t, e)
        for i in (2, 3):
            interleave(i)

        quantize_w_gpsimd()
        interleave_w(2, "s")
        quantize_x(0, 0, E, qt_g[:])
        quantize_x(1, 0, 4, qt[2])
        quantize_x(1, 4, E, qt[3])
        quantize_scalar_pass(3, 0, E)
        for t in range(4):
            for e in range(2):
                scalar_gather(2, t, e)
        interleave_w(3, "s")
        nc.scalar.copy(
            out=wq_of(SHARED[0])[:, SHARED[1], :].rearrange("p (c i t) -> p c t i", i=4, t=4)[:, 0 : SHARED[2]],
            in_=wr[SHARED[0]][:, SHARED[1], :].rearrange("p (t c i) -> p c t i", t=4, i=4)[:, 0 : SHARED[2]],
        )
        for t in range(4):
            for e in range(2, 4):
                scalar_gather(2, t, e)
        for e in range(4, E):
            for t in range(4):
                scalar_gather(2, t, e)
        y = keep.tile([P, S], F32, name="y", tag="xb2")
        interleave_w(3, "v")
        quantize_scalar_pass(2, 0, 2)
        quantize_w(2)
        interleave_w(4, "v")
        quantize_w(3)
        interleave_w(5, "v")
        quantize_scalar_pass(2, 2, 4)
        quantize_w(4)
        interleave_w(6, "v")
        quantize_w(5)
        quantize_w(6)
        interleave_w7(0)
        quantize_scalar_pass(2, 4, 5)
        quantize_scalar_pass(2, 5, 6)
        quantize_w7(0)
        interleave_w7(1)
        quantize_scalar_pass(2, 6, 7)
        quantize_w7(1)
        quantize_scalar_pass(2, 7, 8)

        t1 = keep.tile([P, T], F32, name="t1", tag="gt01")
        t2 = ring.tile([P, T], F32, name="t2", tag="gt", bufs=2)
        res = ring.tile([P, T], F32, name="res", tag="gt", bufs=2)
        nc.vector.tensor_tensor(t1[:], y[:].indirect(pos1_t[:]), gate0[:], MULT)
        for c0 in (0, T // 2):
            cols = slice(c0, c0 + T // 2)
            nc.vector.tensor_tensor(
                t2[:, cols], y[:].indirect(pos2_t[:, c0 // 16 : (c0 + T // 2) // 16]), gate1[:, cols], MULT
            )
        for c0 in (0, T // 2):
            cols = slice(c0, c0 + T // 2)
            nc.vector.tensor_tensor(res[:, cols], t1[:, cols], t2[:, cols], ADD)
            nc.sync.dma_start(out=out[:, cols], in_=res[:, cols])
